import numpy as np
import ml_dtypes


def mxq(x, axis, fmt="e4m3"):
    dtype, down = {"e4m3": (ml_dtypes.float8_e4m3fn, 7), "e5m2": (ml_dtypes.float8_e5m2, 14)}[fmt]
    v = np.moveaxis(np.asarray(x, np.float32).astype(ml_dtypes.bfloat16).astype(np.float64), axis, -1)
    blocks = v.reshape(v.shape[:-1] + (-1, 32))
    amax = np.abs(blocks).max(-1, keepdims=True)
    byte = np.maximum(np.where(amax > 0, np.frexp(amax)[1] - 1 + 127, 0) - down, 1)
    scale = np.exp2(byte - 127.0)
    codes = (blocks / scale).astype(np.float32).astype(dtype).astype(np.float64)
    return np.moveaxis((codes * scale).reshape(v.shape), -1, axis)


WIDE = False


def mx_kscale(k):
    if not WIDE:
        return np.ones(k)
    levels = np.array([10, -10, 5, -5, 0])
    if k % 512:
        return np.exp2(np.random.permutation(np.resize(levels, k // 32))).repeat(32)
    a = np.empty((k // 512, 16))
    for p in range(k // 512):
        a[p, :8] = np.random.permutation(np.resize(levels, 8))
        for g in range(8):
            far = levels[np.abs(levels - a[p, g]) >= 10]
            a[p, g + 8] = far[np.random.randint(len(far))]
    return np.exp2(a.ravel()).repeat(32)


def f64(x):
    return np.asarray(x).astype(np.float64)


def striped(idx):
    return np.tile(idx.reshape(-1, 16).T, (8, 1)).astype(np.uint16)


def unstriped(offs):
    return offs[:16].T.reshape(-1).astype(np.int64)


def pack_weight(w):
    k, n = w.shape
    w = f64(np.asarray(w, np.float32).astype(ml_dtypes.bfloat16)).reshape(k // 32, 32, n)
    amax = np.abs(w).max(1)
    byte = np.clip(np.where(amax > 0, np.frexp(amax)[1] - 1 + 127 - 7, 1), 1, 254)
    scaled = (w * np.exp2(127.0 - byte)[:, None, :]).reshape(k, n).astype(np.float32)
    words = np.ascontiguousarray(scaled.reshape(k // 512, 128, 4, n).transpose(0, 1, 3, 2)).astype(ml_dtypes.float8_e4m3fn).view(np.uint8)
    return words, np.ascontiguousarray(byte.astype(np.uint8).reshape(k // 512, 16, n))


def unpack_weight(words, scales):
    g, p, n, _ = words.shape
    vals = np.ascontiguousarray(words).view(ml_dtypes.float8_e4m3fn).astype(np.float64) * np.repeat(np.exp2(scales.astype(np.float64) - 127.0), 8, axis=1)[..., None]
    return vals.transpose(0, 1, 3, 2).reshape(g * 512, n)


K, T, S, V, H, N = 512, 4096, 1024, 256, 512, 128


def setup_inputs():
    n = np.random.standard_normal
    s = mx_kscale(K)[:, None]
    u = mx_kscale(H)
    packed_w2 = pack_weight(n((H, N)) / np.sqrt(2 * H) / u[:, None])
    packed_w3 = pack_weight(n((H, N)) / np.sqrt(2 * H) / u[:, None])
    return {
        "xT": (n((K, T)) * s).astype(np.float32),
        "w1": (n((K, H)) / np.sqrt(K) / s * u).astype(np.float32),
        "w2_words": packed_w2[0],
        "w2_scales": packed_w2[1],
        "w3_words": packed_w3[0],
        "w3_scales": packed_w3[1],
        "offs": striped(np.random.permutation(T)[:S]),
    }


def reference(xT, w1, w2_words, w2_scales, w3_words, w3_scales, offs):
    xq = mxq(f64(xT)[:, unstriped(offs)], 0, "e4m3")
    h = mxq(f64(w1), 0, "e4m3").T @ xq
    mean = (h[:, :V] + h[:, V:2 * V] + h[:, 2 * V:3 * V] + h[:, 3 * V:4 * V]) / 4
    dev = np.sqrt(((h[:, :V] - mean) ** 2 + (h[:, V:2 * V] - mean) ** 2 + (h[:, 2 * V:3 * V] - mean) ** 2 + (h[:, 3 * V:4 * V] - mean) ** 2) / 4)
    return unpack_weight(w2_words, w2_scales).T @ mxq(mean, 0, "e4m3") + unpack_weight(w3_words, w3_scales).T @ mxq(dev, 0, "e4m3")

@@ -1,0 +1,164 @@
+import math
+from contextlib import ExitStack
+
+import concourse.mybir as mybir
+
+K, T, S, V, H, N = 512, 4096, 1024, 256, 512, 128
+FLOPS = 2 * K * H * S + 2 * 2 * H * N * V
+
+F32 = mybir.dt.float32
+BF16 = mybir.dt.bfloat16
+I32 = mybir.dt.int32
+U32 = mybir.dt.uint32
+U16 = mybir.dt.uint16
+U8 = mybir.dt.uint8
+FP8X4 = mybir.dt.float8_e4m3fn_x4
+ACT = mybir.ActivationFunctionType
+ALU = mybir.AluOpType
+
+P = 128
+PACK = 4
+HALF = S // 2
+VH = 128
+
+
+def tile_picked_statpool_none_e_kernel(tc, xT, w1, w2_words, w2_scales, w3_words, w3_scales, offs, out):
+    nc = tc.nc
+    with ExitStack() as ctx:
+        keep = ctx.enter_context(tc.tile_pool(name="keep", bufs=1))
+        psum = ctx.enter_context(tc.psum_pool(name="psum", bufs=1))
+
+        offsets = keep.tile([P, S // 16], U16, name="offsets")
+        nc.sync.dma_start(offsets[:], offs)
+        w_raw = keep.tile([P, PACK, H], F32, name="w_raw")
+        nc.sync.dma_start(out=w_raw[:], in_=w1.rearrange("(p j) c -> p j c", j=PACK))
+        x_rows = xT.rearrange("(p j) t -> p j t", j=PACK)
+        planes = []
+        for j in range(PACK):
+            plane = keep.tile([P, T], F32, name="plane%d" % j)
+            nc.sync.dma_start(out=plane[:], in_=x_rows[:, j, :])
+            planes.append(plane)
+
+        tail_words = []
+        tail_scales = []
+        for i, (words, scales) in enumerate(((w2_words, w2_scales), (w3_words, w3_scales))):
+            wt = keep.tile([P, N], I32, name="tail_words%d" % i, align_bytes=64)
+            nc.sync.dma_start(out=wt[:], in_=words[0].rearrange("p n t -> p (n t)").bitcast(I32))
+            tail_words.append(wt)
+        for i, (words, scales) in enumerate(((w2_words, w2_scales), (w3_words, w3_scales))):
+            st = keep.tile([P, N], U8, name="tail_scales%d" % i, align_bytes=64)
+            nc.gpsimd.memset(st[:], 0)
+            for q in range(4):
+                nc.sync.dma_start(out=st[32 * q : 32 * q + 4, :].bitcast(I32), in_=scales[0, 4 * q : 4 * q + 4, :].bitcast(I32))
+            tail_scales.append(st)
+
+        warm = keep.tile([P, 2], F32, name="warm")
+        nc.gpsimd.memset(warm[:, 0:1], 1.0)
+        nc.scalar.activation(out=warm[:, 1:2], in_=warm[:, 0:1], func=ACT.Sqrt)
+
+        w_grouped = keep.tile([P, PACK, P, PACK], BF16, name="w_grouped", align_bytes=64)
+        nc.vector.tensor_copy(
+            out=w_grouped[:].rearrange("p t m j -> p m j t"),
+            in_=w_raw[:].rearrange("p j (m t) -> p m j t", t=PACK),
+        )
+        w_codes = keep.tile([P, H], U32, name="w_codes", align_bytes=64)
+        w_scales = keep.tile([P, H], U8, name="w_scales", align_bytes=64)
+        nc.vector.quantize_mx(out=w_codes[:].bitcast(FP8X4), scales=w_scales[:], in_=w_grouped[:].rearrange("p t m j -> p (t m j)"))
+
+        picked = [keep.tile([P, HALF, PACK], BF16, name="picked%d" % h, align_bytes=64) for h in range(2)]
+        x_codes = [keep.tile([P, HALF], U32, name="x_codes%d" % h, align_bytes=64) for h in range(2)]
+        x_scales = [keep.tile([P, HALF], U8, name="x_scales%d" % h, align_bytes=64) for h in range(2)]
+
+        def gather(j, h):
+            cols = HALF // 16
+            nc.vector.tensor_copy(out=picked[h][:, :, j], in_=planes[j][:].indirect(offsets[:, h * cols : (h + 1) * cols]))
+
+        def quantize_x(h):
+            nc.vector.quantize_mx(out=x_codes[h][:].bitcast(FP8X4), scales=x_scales[h][:], in_=picked[h][:].rearrange("p s j -> p (s j)"))
+
+        def product(bank, pieces, vh):
+            for t in range(PACK):
+                for n, d in enumerate(pieces):
+                    cols = slice((d % 2) * V + vh * VH, (d % 2) * V + (vh + 1) * VH)
+                    nc.tensor.matmul_mx(
+                        out=bank[:, t, :],
+                        lhsT=w_codes[:, t * P : (t + 1) * P].bitcast(FP8X4),
+                        lhsT_scale=w_scales[:, t * P : (t + 1) * P],
+                        rhs=x_codes[d // 2][:, cols].bitcast(FP8X4),
+                        rhs_scale=x_scales[d // 2][:, cols],
+                        start=(n == 0),
+                        stop=(n == len(pieces) - 1),
+                    )
+
+        def woven(bank):
+            return bank[:].rearrange("p t v -> p v t")
+
+        def work(name):
+            return [keep.tile([P, VH, PACK], F32, name="%s%d" % (name, vh)) for vh in range(2)]
+
+        for j in range(PACK - 1):
+            gather(j, 0)
+            gather(j, 1)
+        gather(PACK - 1, 0)
+        quantize_x(0)
+
+        bank_u = [psum.tile([P, PACK, VH], F32, name="bank_u%d" % vh) for vh in range(2)]
+        bank_a = [psum.tile([P, PACK, VH], F32, name="bank_a%d" % vh, tag="a%d" % vh) for vh in range(2)]
+        bank_c = [psum.tile([P, PACK, VH], F32, name="bank_c%d" % vh) for vh in range(2)]
+        bank_d = [psum.tile([P, PACK, VH], F32, name="bank_d%d" % vh) for vh in range(2)]
+        u4, a2, pd, w4, h2, h3 = work("u4"), work("a2"), work("pd"), work("w4"), work("h2"), work("h3")
+        sp, s2, s3, t12, q = work("sp"), work("s2"), work("s3"), work("t12"), work("q")
+        mean_b = [keep.tile([P, VH, PACK], BF16, name="mean_b%d" % vh, align_bytes=64) for vh in range(2)]
+        dev_b = [keep.tile([P, VH, PACK], BF16, name="dev_b%d" % vh, align_bytes=64) for vh in range(2)]
+
+        for vh in range(2):
+            product(bank_u[vh], (0, 1), vh)
+            nc.scalar.activation(out=u4[vh][:], in_=woven(bank_u[vh]), func=ACT.Copy, scale=0.25)
+        gather(PACK - 1, 1)
+        quantize_x(1)
+        for vh in range(2):
+            product(bank_a[vh], (0,), vh)
+            nc.scalar.activation(out=a2[vh][:], in_=woven(bank_a[vh]), func=ACT.Copy, scale=0.5)
+            product(bank_c[vh], (2,), vh)
+            product(bank_d[vh], (3,), vh)
+            nc.gpsimd.tensor_tensor(out=pd[vh][:], in0=a2[vh][:], in1=u4[vh][:], op=ALU.subtract)
+            nc.scalar.activation(out=sp[vh][:], in_=pd[vh][:], func=ACT.Square, scale=math.sqrt(6.0))
+
+        def stt(dst, bank, factor, other):
+            nc.vector.scalar_tensor_tensor(out=dst[:], in0=woven(bank), scalar=factor, in1=other[:], op0=ALU.mult, op1=ALU.add)
+
+        def quantize_stat(src, name):
+            codes = keep.tile([P, VH], U32, name=name + "_codes", align_bytes=64)
+            scales = keep.tile([P, VH], U8, name=name + "_scales", align_bytes=64)
+            nc.vector.quantize_mx(out=codes[:].bitcast(FP8X4), scales=scales[:], in_=src[:].rearrange("p v t -> p (v t)"))
+            return codes, scales
+
+        for vh in range(2):
+            stt(w4[vh], bank_c[vh], 0.25, u4[vh])
+            stt(h2[vh], bank_c[vh], -0.5, u4[vh])
+            nc.scalar.activation(out=s2[vh][:], in_=h2[vh][:], func=ACT.Square, scale=math.sqrt(2.0))
+            nc.gpsimd.tensor_tensor(out=t12[vh][:], in0=sp[vh][:], in1=s2[vh][:], op=ALU.add)
+            stt(h3[vh], bank_d[vh], -0.75, w4[vh])
+            nc.scalar.activation(out=s3[vh][:], in_=h3[vh][:], func=ACT.Square)
+            stt(mean_b[vh], bank_d[vh], 0.25, w4[vh])
+        for vh in range(2):
+            adder = nc.gpsimd if vh == 0 else nc.vector
+            adder.tensor_tensor(out=q[vh][:], in0=t12[vh][:], in1=s3[vh][:], op=ALU.add)
+            nc.scalar.activation(out=dev_b[vh][:], in_=q[vh][:], func=ACT.Sqrt, scale=1.0 / 3.0)
+        for vh in range(2):
+            mean_q = quantize_stat(mean_b[vh], "mean%d" % vh)
+            dev_q = quantize_stat(dev_b[vh], "dev%d" % vh)
+            acc = psum.tile([P, VH], F32, name="acc%d" % vh, tag="a%d" % vh)
+            for i, (codes, scales) in enumerate((mean_q, dev_q)):
+                nc.tensor.matmul_mx(
+                    out=acc[:],
+                    lhsT=tail_words[i][:].bitcast(FP8X4),
+                    lhsT_scale=tail_scales[i][:],
+                    rhs=codes[:].bitcast(FP8X4),
+                    rhs_scale=scales[:],
+                    start=(i == 0),
+                    stop=(i == 1),
+                )
+            result = keep.tile([P, VH], F32, name="result%d" % vh)
+            nc.scalar.copy(out=result[:], in_=acc[:])
+            nc.sync.dma_start(out=out[:, vh * VH : (vh + 1) * VH], in_=result[:])

@@ -18,7 +18,7 @@ ALU = mybir.AluOpType
 
 P = 128
 PACK = 4
-HALF = S // 2
+D = 4
 VH = 128
 
 
@@ -28,16 +28,17 @@ def tile_picked_statpool_none_e_kernel(tc, xT, w1, w2_words, w2_scales, w3_words
         keep = ctx.enter_context(tc.tile_pool(name="keep", bufs=1))
         psum = ctx.enter_context(tc.psum_pool(name="psum", bufs=1))
 
-        offsets = keep.tile([P, S // 16], U16, name="offsets")
-        nc.sync.dma_start(offsets[:], offs)
-        w_raw = keep.tile([P, PACK, H], F32, name="w_raw")
-        nc.sync.dma_start(out=w_raw[:], in_=w1.rearrange("(p j) c -> p j c", j=PACK))
         x_rows = xT.rearrange("(p j) t -> p j t", j=PACK)
-        planes = []
-        for j in range(PACK):
-            plane = keep.tile([P, T], F32, name="plane%d" % j)
-            nc.sync.dma_start(out=plane[:], in_=x_rows[:, j, :])
-            planes.append(plane)
+        planes = [keep.tile([P, T], F32, name="plane%d" % j) for j in range(PACK)]
+        offsets = keep.tile([P, S // 16], U16, name="offsets")
+        nc.sync.dma_start(out=planes[0][:], in_=x_rows[:, 0, :])
+        nc.sync.dma_start(offsets[:], offs)
+        for j in range(1, PACK):
+            nc.sync.dma_start(out=planes[j][:], in_=x_rows[:, j, :])
+        w_rows = w1.rearrange("(p j) c -> p j c", j=PACK)
+        w_raw = [keep.tile([P, PACK, H // 2], F32, name="w_raw%d" % c) for c in range(2)]
+        for c in range(2):
+            nc.sync.dma_start(out=w_raw[c][:], in_=w_rows[:, :, c * (H // 2) : (c + 1) * (H // 2)])
 
         tail_words = []
         tail_scales = []
@@ -56,36 +57,47 @@ def tile_picked_statpool_none_e_kernel(tc, xT, w1, w2_words, w2_scales, w3_words
         nc.gpsimd.memset(warm[:, 0:1], 1.0)
         nc.scalar.activation(out=warm[:, 1:2], in_=warm[:, 0:1], func=ACT.Sqrt)
 
-        w_grouped = keep.tile([P, PACK, P, PACK], BF16, name="w_grouped", align_bytes=64)
-        nc.vector.tensor_copy(
-            out=w_grouped[:].rearrange("p t m j -> p m j t"),
-            in_=w_raw[:].rearrange("p j (m t) -> p m j t", t=PACK),
-        )
-        w_codes = keep.tile([P, H], U32, name="w_codes", align_bytes=64)
-        w_scales = keep.tile([P, H], U8, name="w_scales", align_bytes=64)
-        nc.vector.quantize_mx(out=w_codes[:].bitcast(FP8X4), scales=w_scales[:], in_=w_grouped[:].rearrange("p t m j -> p (t m j)"))
+        picked = keep.tile([P, 2, D, VH, PACK], BF16, name="picked", align_bytes=64)
+        for j in range(PACK):
+            nc.vector.tensor_copy(out=picked[:, :, :, :, j].rearrange("p h d v -> p d h v"), in_=planes[j][:].indirect(offsets[:]))
 
-        picked = [keep.tile([P, HALF, PACK], BF16, name="picked%d" % h, align_bytes=64) for h in range(2)]
-        x_codes = [keep.tile([P, HALF], U32, name="x_codes%d" % h, align_bytes=64) for h in range(2)]
-        x_scales = [keep.tile([P, HALF], U8, name="x_scales%d" % h, align_bytes=64) for h in range(2)]
+        w_grouped = keep.tile([P, PACK, P, PACK], BF16, name="w_grouped", tag="w_stage", align_bytes=64)
+        for c in range(2):
+            nc.scalar.copy(
+                out=w_grouped[:, :, c * (P // 2) : (c + 1) * (P // 2), :].rearrange("p t m j -> p m j t"),
+                in_=w_raw[c][:].rearrange("p j (m t) -> p m j t", t=PACK),
+            )
 
-        def gather(j, h):
-            cols = HALF // 16
-            nc.vector.tensor_copy(out=picked[h][:, :, j], in_=planes[j][:].indirect(offsets[:, h * cols : (h + 1) * cols]))
+        def quantize(src, width, name, tag=""):
+            codes = keep.tile([P, width], U32, name=name + "_codes", tag=tag, align_bytes=64)
+            scales = keep.tile([P, width], U8, name=name + "_scales", align_bytes=64)
+            nc.vector.quantize_mx(out=codes[:].bitcast(FP8X4), scales=scales[:], in_=src)
+            return codes, scales
 
-        def quantize_x(h):
-            nc.vector.quantize_mx(out=x_codes[h][:].bitcast(FP8X4), scales=x_scales[h][:], in_=picked[h][:].rearrange("p s j -> p (s j)"))
+        x_ab0 = quantize(picked[:, 0, 0:2].rearrange("p d v j -> p (d v j)"), 2 * VH, "x_ab0")
+        w_q = [quantize(w_grouped[:, t].rearrange("p m j -> p (m j)"), P, "w%d" % t) for t in range(PACK)]
+        x_cd0 = quantize(picked[:, 0, 2:4].rearrange("p d v j -> p (d v j)"), 2 * VH, "x_cd0")
+        x_1 = quantize(picked[:, 1].rearrange("p d v j -> p (d v j)"), D * VH, "x_1", tag="w_stage")
+
+        def moving(d, vh):
+            if vh == 1:
+                codes, scales, at = x_1[0], x_1[1], d
+            else:
+                codes, scales = x_ab0 if d < 2 else x_cd0
+                at = d % 2
+            cols = slice(at * VH, (at + 1) * VH)
+            return codes[:, cols].bitcast(FP8X4), scales[:, cols]
 
         def product(bank, pieces, vh):
             for t in range(PACK):
                 for n, d in enumerate(pieces):
-                    cols = slice((d % 2) * V + vh * VH, (d % 2) * V + (vh + 1) * VH)
+                    rhs, rhs_scale = moving(d, vh)
                     nc.tensor.matmul_mx(
                         out=bank[:, t, :],
-                        lhsT=w_codes[:, t * P : (t + 1) * P].bitcast(FP8X4),
-                        lhsT_scale=w_scales[:, t * P : (t + 1) * P],
-                        rhs=x_codes[d // 2][:, cols].bitcast(FP8X4),
-                        rhs_scale=x_scales[d // 2][:, cols],
+                        lhsT=w_q[t][0][:].bitcast(FP8X4),
+                        lhsT_scale=w_q[t][1][:],
+                        rhs=rhs,
+                        rhs_scale=rhs_scale,
                         start=(n == 0),
                         stop=(n == len(pieces) - 1),
                     )
@@ -93,72 +105,83 @@ def tile_picked_statpool_none_e_kernel(tc, xT, w1, w2_words, w2_scales, w3_words
         def woven(bank):
             return bank[:].rearrange("p t v -> p v t")
 
-        def work(name):
-            return [keep.tile([P, VH, PACK], F32, name="%s%d" % (name, vh)) for vh in range(2)]
+        def work(name, tag=""):
+            return keep.tile([P, VH, PACK], F32, name=name, tag=tag, align_bytes=64)
 
-        for j in range(PACK - 1):
-            gather(j, 0)
-            gather(j, 1)
-        gather(PACK - 1, 0)
-        quantize_x(0)
+        def bank(name, tag=""):
+            return psum.tile([P, PACK, VH], F32, name=name, tag=tag)
 
-        bank_u = [psum.tile([P, PACK, VH], F32, name="bank_u%d" % vh) for vh in range(2)]
-        bank_a = [psum.tile([P, PACK, VH], F32, name="bank_a%d" % vh, tag="a%d" % vh) for vh in range(2)]
-        bank_c = [psum.tile([P, PACK, VH], F32, name="bank_c%d" % vh) for vh in range(2)]
-        bank_d = [psum.tile([P, PACK, VH], F32, name="bank_d%d" % vh) for vh in range(2)]
-        u4, a2, pd, w4, h2, h3 = work("u4"), work("a2"), work("pd"), work("w4"), work("h2"), work("h3")
-        sp, s2, s3, t12, q = work("sp"), work("s2"), work("s3"), work("t12"), work("q")
-        mean_b = [keep.tile([P, VH, PACK], BF16, name="mean_b%d" % vh, align_bytes=64) for vh in range(2)]
-        dev_b = [keep.tile([P, VH, PACK], BF16, name="dev_b%d" % vh, align_bytes=64) for vh in range(2)]
+        def stt(dst, src, factor, other, op1=ALU.add):
+            nc.vector.scalar_tensor_tensor(out=dst, in0=woven(src), scalar=factor, in1=other[:], op0=ALU.mult, op1=op1)
 
+        bank_u = [bank("bank_u%d" % vh) for vh in range(2)]
+        bank_a = [bank("bank_a%d" % vh, "a%d" % vh) for vh in range(2)]
+        bank_c = [bank("bank_c%d" % vh) for vh in range(2)]
+        bank_d = [bank("bank_d%d" % vh) for vh in range(2)]
+        u4 = [work("u4_%d" % vh) for vh in range(2)]
+
+        product(bank_u[0], (0, 1), 0)
+        nc.scalar.activation(out=u4[0][:], in_=woven(bank_u[0]), func=ACT.Copy, scale=0.25)
+        product(bank_c[0], (2,), 0)
+        product(bank_u[1], (0, 1), 1)
+        nc.scalar.activation(out=u4[1][:], in_=woven(bank_u[1]), func=ACT.Copy, scale=0.25)
+        product(bank_a[0], (0,), 0)
+        product(bank_d[0], (3,), 0)
+        product(bank_c[1], (2,), 1)
+        product(bank_a[1], (0,), 1)
+        product(bank_d[1], (3,), 1)
+
+        w4, sp, s2, s3 = [], [], [], []
+        q = [work("q%d" % vh) for vh in range(2)]
         for vh in range(2):
-            product(bank_u[vh], (0, 1), vh)
-            nc.scalar.activation(out=u4[vh][:], in_=woven(bank_u[vh]), func=ACT.Copy, scale=0.25)
-        gather(PACK - 1, 1)
-        quantize_x(1)
-        for vh in range(2):
-            product(bank_a[vh], (0,), vh)
-            nc.scalar.activation(out=a2[vh][:], in_=woven(bank_a[vh]), func=ACT.Copy, scale=0.5)
-            product(bank_c[vh], (2,), vh)
-            product(bank_d[vh], (3,), vh)
-            nc.gpsimd.tensor_tensor(out=pd[vh][:], in0=a2[vh][:], in1=u4[vh][:], op=ALU.subtract)
-            nc.scalar.activation(out=sp[vh][:], in_=pd[vh][:], func=ACT.Square, scale=math.sqrt(6.0))
+            w4.append(work("w4_%d" % vh))
+            stt(w4[vh][:], bank_c[vh], 0.25, u4[vh])
+            h2 = work("h2_%d" % vh)
+            stt(h2[:], bank_c[vh], -0.5, u4[vh])
+            s2.append(work("s2_%d" % vh))
+            nc.scalar.activation(out=s2[vh][:], in_=h2[:], func=ACT.Square, scale=math.sqrt(2.0))
+            pd = work("pd_%d" % vh)
+            stt(pd[:], bank_a[vh], 0.5, u4[vh], ALU.subtract)
+            sp.append(work("sp_%d" % vh))
+            nc.scalar.activation(out=sp[vh][:], in_=pd[:], func=ACT.Square, scale=math.sqrt(6.0))
+            h3 = work("h3_%d" % vh, "h3_%d" % vh)
+            stt(h3[:], bank_d[vh], -0.75, w4[vh])
+            s3.append(work("s3_%d" % vh, "s3_%d" % vh))
+            nc.scalar.activation(out=s3[vh][:], in_=h3[:], func=ACT.Square)
+            if vh == 0:
+                t12 = work("t12_0", "t12")
+                nc.gpsimd.tensor_tensor(out=t12[:], in0=sp[0][:], in1=s2[0][:], op=ALU.add)
+                nc.gpsimd.tensor_tensor(out=q[0][:], in0=t12[:], in1=s3[0][:], op=ALU.add)
 
-        def stt(dst, bank, factor, other):
-            nc.vector.scalar_tensor_tensor(out=dst[:], in0=woven(bank), scalar=factor, in1=other[:], op0=ALU.mult, op1=ALU.add)
-
-        def quantize_stat(src, name):
-            codes = keep.tile([P, VH], U32, name=name + "_codes", align_bytes=64)
-            scales = keep.tile([P, VH], U8, name=name + "_scales", align_bytes=64)
-            nc.vector.quantize_mx(out=codes[:].bitcast(FP8X4), scales=scales[:], in_=src[:].rearrange("p v t -> p (v t)"))
-            return codes, scales
-
+        mean_b = keep.tile([P, 2, VH, PACK], BF16, name="mean_b", align_bytes=64)
         for vh in range(2):
-            stt(w4[vh], bank_c[vh], 0.25, u4[vh])
-            stt(h2[vh], bank_c[vh], -0.5, u4[vh])
-            nc.scalar.activation(out=s2[vh][:], in_=h2[vh][:], func=ACT.Square, scale=math.sqrt(2.0))
-            nc.gpsimd.tensor_tensor(out=t12[vh][:], in0=sp[vh][:], in1=s2[vh][:], op=ALU.add)
-            stt(h3[vh], bank_d[vh], -0.75, w4[vh])
-            nc.scalar.activation(out=s3[vh][:], in_=h3[vh][:], func=ACT.Square)
-            stt(mean_b[vh], bank_d[vh], 0.25, w4[vh])
+            stt(mean_b[:, vh], bank_d[vh], 0.25, w4[vh])
+        t12 = work("t12_1", "t12")
+        nc.vector.tensor_tensor(out=t12[:], in0=sp[1][:], in1=s2[1][:], op=ALU.add)
+        mean_q = quantize(mean_b[:].rearrange("p h v t -> p (h v t)"), 2 * VH, "mean", tag="s3_0")
+        dev_b = [
+            keep.tile([P, VH, PACK], BF16, name="dev_b0", tag="h3_1", align_bytes=64),
+            keep.tile([P, VH, PACK], BF16, name="dev_b1", align_bytes=64),
+        ]
+        nc.scalar.activation(out=dev_b[0][:], in_=q[0][:], func=ACT.Sqrt, scale=1.0 / 3.0)
+        for c in range(2):
+            cols = slice(c * VH // 2, (c + 1) * VH // 2)
+            nc.vector.tensor_tensor(out=q[1][:, cols], in0=t12[:, cols], in1=s3[1][:, cols], op=ALU.add)
+            nc.scalar.activation(out=dev_b[1][:, cols], in_=q[1][:, cols], func=ACT.Sqrt, scale=1.0 / 3.0)
         for vh in range(2):
-            adder = nc.gpsimd if vh == 0 else nc.vector
-            adder.tensor_tensor(out=q[vh][:], in0=t12[vh][:], in1=s3[vh][:], op=ALU.add)
-            nc.scalar.activation(out=dev_b[vh][:], in_=q[vh][:], func=ACT.Sqrt, scale=1.0 / 3.0)
-        for vh in range(2):
-            mean_q = quantize_stat(mean_b[vh], "mean%d" % vh)
-            dev_q = quantize_stat(dev_b[vh], "dev%d" % vh)
+            dev_q = quantize(dev_b[vh][:].rearrange("p v t -> p (v t)"), VH, "dev%d" % vh)
+            cols = slice(vh * VH, (vh + 1) * VH)
             acc = psum.tile([P, VH], F32, name="acc%d" % vh, tag="a%d" % vh)
-            for i, (codes, scales) in enumerate((mean_q, dev_q)):
+            for i, (codes, scales) in enumerate(((mean_q[0][:, cols], mean_q[1][:, cols]), (dev_q[0][:], dev_q[1][:]))):
                 nc.tensor.matmul_mx(
                     out=acc[:],
                     lhsT=tail_words[i][:].bitcast(FP8X4),
                     lhsT_scale=tail_scales[i][:],
-                    rhs=codes[:].bitcast(FP8X4),
-                    rhs_scale=scales[:],
+                    rhs=codes.bitcast(FP8X4),
+                    rhs_scale=scales,
                     start=(i == 0),
                     stop=(i == 1),
                 )
             result = keep.tile([P, VH], F32, name="result%d" % vh)
             nc.scalar.copy(out=result[:], in_=acc[:])
-            nc.sync.dma_start(out=out[:, vh * VH : (vh + 1) * VH], in_=result[:])
+            nc.sync.dma_start(out=out[:, cols], in_=result[:])

@@ -36,9 +36,9 @@ def tile_picked_statpool_none_e_kernel(tc, xT, w1, w2_words, w2_scales, w3_words
         for j in range(1, PACK):
             nc.sync.dma_start(out=planes[j][:], in_=x_rows[:, j, :])
         w_rows = w1.rearrange("(p j) c -> p j c", j=PACK)
-        w_raw = [keep.tile([P, PACK, H // 2], F32, name="w_raw%d" % c) for c in range(2)]
-        for c in range(2):
-            nc.sync.dma_start(out=w_raw[c][:], in_=w_rows[:, :, c * (H // 2) : (c + 1) * (H // 2)])
+        w_raw = [keep.tile([P, PACK, H // 4], F32, name="w_raw%d" % c, tag="w_raw%d" % c, align_bytes=64) for c in range(4)]
+        for c in range(4):
+            nc.sync.dma_start(out=w_raw[c][:], in_=w_rows[:, :, c * (H // 4) : (c + 1) * (H // 4)])
 
         tail_words = []
         tail_scales = []
@@ -58,13 +58,18 @@ def tile_picked_statpool_none_e_kernel(tc, xT, w1, w2_words, w2_scales, w3_words
         nc.scalar.activation(out=warm[:, 1:2], in_=warm[:, 0:1], func=ACT.Sqrt)
 
         picked = keep.tile([P, 2, D, VH, PACK], BF16, name="picked", align_bytes=64)
-        for j in range(PACK):
+        for j in range(PACK - 1):
             nc.vector.tensor_copy(out=picked[:, :, :, :, j].rearrange("p h d v -> p d h v"), in_=planes[j][:].indirect(offsets[:]))
+        for pair in range(2):
+            nc.vector.tensor_copy(
+                out=picked[:, :, 2 * pair : 2 * pair + 2, :, PACK - 1].rearrange("p h d v -> p d h v"),
+                in_=planes[PACK - 1][:].indirect(offsets[:, pair * 32 : (pair + 1) * 32]),
+            )
 
         w_grouped = keep.tile([P, PACK, P, PACK], BF16, name="w_grouped", tag="w_stage", align_bytes=64)
-        for c in range(2):
+        for c in range(4):
             nc.scalar.copy(
-                out=w_grouped[:, :, c * (P // 2) : (c + 1) * (P // 2), :].rearrange("p t m j -> p m j t"),
+                out=w_grouped[:, :, c * (P // 4) : (c + 1) * (P // 4), :].rearrange("p t m j -> p m j t"),
                 in_=w_raw[c][:].rearrange("p j (m t) -> p m j t", t=PACK),
             )
 
@@ -76,7 +81,7 @@ def tile_picked_statpool_none_e_kernel(tc, xT, w1, w2_words, w2_scales, w3_words
 
         x_ab0 = quantize(picked[:, 0, 0:2].rearrange("p d v j -> p (d v j)"), 2 * VH, "x_ab0")
         w_q = [quantize(w_grouped[:, t].rearrange("p m j -> p (m j)"), P, "w%d" % t) for t in range(PACK)]
-        x_cd0 = quantize(picked[:, 0, 2:4].rearrange("p d v j -> p (d v j)"), 2 * VH, "x_cd0")
+        x_cd0 = quantize(picked[:, 0, 2:4].rearrange("p d v j -> p (d v j)"), 2 * VH, "x_cd0", tag="w_raw3")
         x_1 = quantize(picked[:, 1].rearrange("p d v j -> p (d v j)"), D * VH, "x_1", tag="w_stage")
 
         def moving(d, vh):
@@ -149,16 +154,17 @@ def tile_picked_statpool_none_e_kernel(tc, xT, w1, w2_words, w2_scales, w3_words
             s3.append(work("s3_%d" % vh, "s3_%d" % vh))
             nc.scalar.activation(out=s3[vh][:], in_=h3[:], func=ACT.Square)
             if vh == 0:
-                t12 = work("t12_0", "t12")
+                t12 = work("t12_0")
                 nc.gpsimd.tensor_tensor(out=t12[:], in0=sp[0][:], in1=s2[0][:], op=ALU.add)
                 nc.gpsimd.tensor_tensor(out=q[0][:], in0=t12[:], in1=s3[0][:], op=ALU.add)
 
         mean_b = keep.tile([P, 2, VH, PACK], BF16, name="mean_b", align_bytes=64)
         for vh in range(2):
             stt(mean_b[:, vh], bank_d[vh], 0.25, w4[vh])
-        t12 = work("t12_1", "t12")
-        nc.vector.tensor_tensor(out=t12[:], in0=sp[1][:], in1=s2[1][:], op=ALU.add)
-        mean_q = quantize(mean_b[:].rearrange("p h v t -> p (h v t)"), 2 * VH, "mean", tag="s3_0")
+        t12 = work("t12_1")
+        for c in range(2):
+            cols = slice(c * VH // 2, (c + 1) * VH // 2)
+            nc.vector.tensor_tensor(out=t12[:, cols], in0=sp[1][:, cols], in1=s2[1][:, cols], op=ALU.add)
         dev_b = [
             keep.tile([P, VH, PACK], BF16, name="dev_b0", tag="h3_1", align_bytes=64),
             keep.tile([P, VH, PACK], BF16, name="dev_b1", align_bytes=64),
@@ -168,6 +174,7 @@ def tile_picked_statpool_none_e_kernel(tc, xT, w1, w2_words, w2_scales, w3_words
             cols = slice(c * VH // 2, (c + 1) * VH // 2)
             nc.vector.tensor_tensor(out=q[1][:, cols], in0=t12[:, cols], in1=s3[1][:, cols], op=ALU.add)
             nc.scalar.activation(out=dev_b[1][:, cols], in_=q[1][:, cols], func=ACT.Sqrt, scale=1.0 / 3.0)
+        mean_q = quantize(mean_b[:].rearrange("p h v t -> p (h v t)"), 2 * VH, "mean", tag="s3_1")
         for vh in range(2):
             dev_q = quantize(dev_b[vh][:].rearrange("p v t -> p (v t)"), VH, "dev%d" % vh)
             cols = slice(vh * VH, (vh + 1) * VH)

@@ -67,11 +67,16 @@ def tile_picked_statpool_none_e_kernel(tc, xT, w1, w2_words, w2_scales, w3_words
             )
 
         w_grouped = keep.tile([P, PACK, P, PACK], BF16, name="w_grouped", tag="w_stage", align_bytes=64)
-        for c in range(4):
+        def cast(c, slots):
             nc.scalar.copy(
-                out=w_grouped[:, :, c * (P // 4) : (c + 1) * (P // 4), :].rearrange("p t m j -> p m j t"),
-                in_=w_raw[c][:].rearrange("p j (m t) -> p m j t", t=PACK),
+                out=w_grouped[:, slots, c * (P // 4) : (c + 1) * (P // 4), :].rearrange("p t m j -> p m j t"),
+                in_=w_raw[c][:].rearrange("p j (m t) -> p m j t", t=PACK)[:, :, :, slots],
             )
+
+        for c in range(3):
+            cast(c, slice(0, PACK))
+        cast(3, slice(0, 2))
+        cast(3, slice(2, PACK))
 
         def quantize(src, width, name, tag=""):
             codes = keep.tile([P, width], U32, name=name + "_codes", tag=tag, align_bytes=64)
@@ -151,12 +156,18 @@ def tile_picked_statpool_none_e_kernel(tc, xT, w1, w2_words, w2_scales, w3_words
             nc.scalar.activation(out=sp[vh][:], in_=pd[:], func=ACT.Square, scale=math.sqrt(6.0))
             h3 = work("h3_%d" % vh, "h3_%d" % vh)
             stt(h3[:], bank_d[vh], -0.75, w4[vh])
-            s3.append(work("s3_%d" % vh, "s3_%d" % vh))
-            nc.scalar.activation(out=s3[vh][:], in_=h3[:], func=ACT.Square)
+            if vh == 1:
+                s3_last = [keep.tile([P, VH // 2, PACK], F32, name="s3_1_%d" % c, tag="s3_1_%d" % c, align_bytes=64) for c in range(2)]
+                for c in range(2):
+                    nc.scalar.activation(out=s3_last[c][:], in_=h3[:, c * VH // 2 : (c + 1) * VH // 2], func=ACT.Square)
             if vh == 0:
+                s3.append(work("s3_0"))
+                nc.scalar.activation(out=s3[0][:], in_=h3[:], func=ACT.Square)
                 t12 = work("t12_0")
                 nc.gpsimd.tensor_tensor(out=t12[:], in0=sp[0][:], in1=s2[0][:], op=ALU.add)
-                nc.gpsimd.tensor_tensor(out=q[0][:], in0=t12[:], in1=s3[0][:], op=ALU.add)
+                first_parts = (slice(0, 3 * VH // 4), slice(3 * VH // 4, VH))
+                for cols in first_parts:
+                    nc.gpsimd.tensor_tensor(out=q[0][:, cols], in0=t12[:, cols], in1=s3[0][:, cols], op=ALU.add)
 
         mean_b = keep.tile([P, 2, VH, PACK], BF16, name="mean_b", align_bytes=64)
         for vh in range(2):
@@ -169,14 +180,29 @@ def tile_picked_statpool_none_e_kernel(tc, xT, w1, w2_words, w2_scales, w3_words
             keep.tile([P, VH, PACK], BF16, name="dev_b0", tag="h3_1", align_bytes=64),
             keep.tile([P, VH, PACK], BF16, name="dev_b1", align_bytes=64),
         ]
-        nc.scalar.activation(out=dev_b[0][:], in_=q[0][:], func=ACT.Sqrt, scale=1.0 / 3.0)
-        for c in range(2):
-            cols = slice(c * VH // 2, (c + 1) * VH // 2)
-            nc.vector.tensor_tensor(out=q[1][:, cols], in0=t12[:, cols], in1=s3[1][:, cols], op=ALU.add)
+        for cols in first_parts:
+            nc.scalar.activation(out=dev_b[0][:, cols], in_=q[0][:, cols], func=ACT.Sqrt, scale=1.0 / 3.0)
+        for c in range(4):
+            cols = slice(c * VH // 4, (c + 1) * VH // 4)
+            part = slice(c % 2 * VH // 4, (c % 2 + 1) * VH // 4)
+            nc.vector.tensor_tensor(out=q[1][:, cols], in0=t12[:, cols], in1=s3_last[c // 2][:, part], op=ALU.add)
             nc.scalar.activation(out=dev_b[1][:, cols], in_=q[1][:, cols], func=ACT.Sqrt, scale=1.0 / 3.0)
-        mean_q = quantize(mean_b[:].rearrange("p h v t -> p (h v t)"), 2 * VH, "mean", tag="s3_1")
+        mean_q = quantize(mean_b[:].rearrange("p h v t -> p (h v t)"), 2 * VH, "mean", tag="s3_1_0")
         for vh in range(2):
-            dev_q = quantize(dev_b[vh][:].rearrange("p v t -> p (v t)"), VH, "dev%d" % vh)
+            if vh == 0:
+                dev_q = quantize(dev_b[vh][:].rearrange("p v t -> p (v t)"), VH, "dev%d" % vh)
+            else:
+                dev_q = (
+                    keep.tile([P, VH], U32, name="dev1_codes", align_bytes=64),
+                    keep.tile([P, VH], U8, name="dev1_scales", align_bytes=64),
+                )
+                for c in range(2):
+                    part = slice(c * VH // 2, (c + 1) * VH // 2)
+                    nc.vector.quantize_mx(
+                        out=dev_q[0][:, part].bitcast(FP8X4),
+                        scales=dev_q[1][:, part],
+                        in_=dev_b[1][:, part].rearrange("p v t -> p (v t)"),
+                    )
             cols = slice(vh * VH, (vh + 1) * VH)
             acc = psum.tile([P, VH], F32, name="acc%d" % vh, tag="a%d" % vh)
             for i, (codes, scales) in enumerate(((mean_q[0][:, cols], mean_q[1][:, cols]), (dev_q[0][:], dev_q[1][:]))):

@@ -57,16 +57,18 @@ def tile_picked_statpool_none_e_kernel(tc, xT, w1, w2_words, w2_scales, w3_words
         nc.gpsimd.memset(warm[:, 0:1], 1.0)
         nc.scalar.activation(out=warm[:, 1:2], in_=warm[:, 0:1], func=ACT.Sqrt)
 
-        picked = keep.tile([P, 2, D, VH, PACK], BF16, name="picked", align_bytes=64)
+        stage = keep.tile([P, 3, D * VH * PACK], BF16, name="stage", align_bytes=64)
+        picked = stage[:, 0:3:2, :].rearrange("p h (d v j) -> p h d v j", d=D, j=PACK)
+        w_grouped = stage[:, 1, :].rearrange("p (t m j) -> p t m j", t=PACK, j=PACK)
         for j in range(PACK - 1):
             nc.vector.tensor_copy(out=picked[:, :, :, :, j].rearrange("p h d v -> p d h v"), in_=planes[j][:].indirect(offsets[:]))
-        for pair in range(2):
-            nc.vector.tensor_copy(
-                out=picked[:, :, 2 * pair : 2 * pair + 2, :, PACK - 1].rearrange("p h d v -> p d h v"),
-                in_=planes[PACK - 1][:].indirect(offsets[:, pair * 32 : (pair + 1) * 32]),
-            )
+        nc.vector.tensor_copy(
+            out=picked[:, :, 0:2, :, PACK - 1].rearrange("p h d v -> p d h v"),
+            in_=planes[PACK - 1][:].indirect(offsets[:, 0:32]),
+        )
+        last = keep.tile([P, 2, 2, VH], BF16, name="last", align_bytes=64)
+        nc.vector.tensor_copy(out=last[:].rearrange("p d h v -> p (d h v)"), in_=planes[PACK - 1][:].indirect(offsets[:, 32:64]))
 
-        w_grouped = keep.tile([P, PACK, P, PACK], BF16, name="w_grouped", tag="w_stage", align_bytes=64)
         def cast(c, slots):
             nc.scalar.copy(
                 out=w_grouped[:, slots, c * (P // 4) : (c + 1) * (P // 4), :].rearrange("p t m j -> p m j t"),
@@ -86,15 +88,18 @@ def tile_picked_statpool_none_e_kernel(tc, xT, w1, w2_words, w2_scales, w3_words
 
         x_ab0 = quantize(picked[:, 0, 0:2].rearrange("p d v j -> p (d v j)"), 2 * VH, "x_ab0")
         w_q = [quantize(w_grouped[:, t].rearrange("p m j -> p (m j)"), P, "w%d" % t) for t in range(PACK)]
-        x_cd0 = quantize(picked[:, 0, 2:4].rearrange("p d v j -> p (d v j)"), 2 * VH, "x_cd0", tag="w_raw3")
-        x_1 = quantize(picked[:, 1].rearrange("p d v j -> p (d v j)"), D * VH, "x_1", tag="w_stage")
+        for d in range(2):
+            nc.vector.tensor_copy(out=picked[:, :, 2 + d, :, PACK - 1], in_=last[:, d])
+        x_c0 = quantize(picked[:, 0, 2].rearrange("p v j -> p (v j)"), VH, "x_c0")
+        x_ab1 = quantize(picked[:, 1, 0:2].rearrange("p d v j -> p (d v j)"), 2 * VH, "x_ab1", tag="w_raw3")
+        x_d0 = quantize(picked[:, 0, 3].rearrange("p v j -> p (v j)"), VH, "x_d0")
+        x_cd1 = quantize(picked[:, 1, 2:4].rearrange("p d v j -> p (d v j)"), 2 * VH, "x_cd1")
 
         def moving(d, vh):
-            if vh == 1:
-                codes, scales, at = x_1[0], x_1[1], d
+            if vh == 0 and d >= 2:
+                (codes, scales), at = (x_c0, x_d0)[d - 2], 0
             else:
-                codes, scales = x_ab0 if d < 2 else x_cd0
-                at = d % 2
+                (codes, scales), at = ((x_ab0, None), (x_ab1, x_cd1))[vh][d // 2], d % 2
             cols = slice(at * VH, (at + 1) * VH)
             return codes[:, cols].bitcast(FP8X4), scales[:, cols]
 
@@ -132,10 +137,10 @@ def tile_picked_statpool_none_e_kernel(tc, xT, w1, w2_words, w2_scales, w3_words
 
         product(bank_u[0], (0, 1), 0)
         nc.scalar.activation(out=u4[0][:], in_=woven(bank_u[0]), func=ACT.Copy, scale=0.25)
+        product(bank_a[0], (0,), 0)
         product(bank_c[0], (2,), 0)
         product(bank_u[1], (0, 1), 1)
         nc.scalar.activation(out=u4[1][:], in_=woven(bank_u[1]), func=ACT.Copy, scale=0.25)
-        product(bank_a[0], (0,), 0)
         product(bank_d[0], (3,), 0)
         product(bank_c[1], (2,), 1)
         product(bank_a[1], (0,), 1)
@@ -144,16 +149,16 @@ def tile_picked_statpool_none_e_kernel(tc, xT, w1, w2_words, w2_scales, w3_words
         w4, sp, s2, s3 = [], [], [], []
         q = [work("q%d" % vh) for vh in range(2)]
         for vh in range(2):
+            pd = work("pd_%d" % vh)
+            stt(pd[:], bank_a[vh], 0.5, u4[vh], ALU.subtract)
+            sp.append(work("sp_%d" % vh))
+            nc.scalar.activation(out=sp[vh][:], in_=pd[:], func=ACT.Square, scale=math.sqrt(6.0))
             w4.append(work("w4_%d" % vh))
             stt(w4[vh][:], bank_c[vh], 0.25, u4[vh])
             h2 = work("h2_%d" % vh)
             stt(h2[:], bank_c[vh], -0.5, u4[vh])
             s2.append(work("s2_%d" % vh))
             nc.scalar.activation(out=s2[vh][:], in_=h2[:], func=ACT.Square, scale=math.sqrt(2.0))
-            pd = work("pd_%d" % vh)
-            stt(pd[:], bank_a[vh], 0.5, u4[vh], ALU.subtract)
-            sp.append(work("sp_%d" % vh))
-            nc.scalar.activation(out=sp[vh][:], in_=pd[:], func=ACT.Square, scale=math.sqrt(6.0))
             h3 = work("h3_%d" % vh, "h3_%d" % vh)
             stt(h3[:], bank_d[vh], -0.75, w4[vh])
             if vh == 1:
@@ -172,7 +177,7 @@ def tile_picked_statpool_none_e_kernel(tc, xT, w1, w2_words, w2_scales, w3_words
         mean_b = keep.tile([P, 2, VH, PACK], BF16, name="mean_b", align_bytes=64)
         for vh in range(2):
             stt(mean_b[:, vh], bank_d[vh], 0.25, w4[vh])
-        t12 = work("t12_1")
+        t12 = work("t12_1", "t12_1")
         for c in range(2):
             cols = slice(c * VH // 2, (c + 1) * VH // 2)
             nc.vector.tensor_tensor(out=t12[:, cols], in0=sp[1][:, cols], in1=s2[1][:, cols], op=ALU.add)
@@ -190,7 +195,7 @@ def tile_picked_statpool_none_e_kernel(tc, xT, w1, w2_words, w2_scales, w3_words
         mean_q = quantize(mean_b[:].rearrange("p h v t -> p (h v t)"), 2 * VH, "mean", tag="s3_1_0")
         for vh in range(2):
             if vh == 0:
-                dev_q = quantize(dev_b[vh][:].rearrange("p v t -> p (v t)"), VH, "dev%d" % vh)
+                dev_q = quantize(dev_b[vh][:].rearrange("p v t -> p (v t)"), VH, "dev0", tag="t12_1")
             else:
                 dev_q = (
                     keep.tile([P, VH], U32, name="dev1_codes", align_bytes=64),

@@ -20,6 +20,12 @@ P = 128
 PACK = 4
 D = 4
 VH = 128
+W_CHUNKS = 4
+QUADRANTS = 4
+
+
+def parts(n):
+    return [slice(c * VH // n, (c + 1) * VH // n) for c in range(n)]
 
 
 def tile_picked_statpool_none_e_kernel(tc, xT, w1, w2_words, w2_scales, w3_words, w3_scales, offs, out):
@@ -36,104 +42,114 @@ def tile_picked_statpool_none_e_kernel(tc, xT, w1, w2_words, w2_scales, w3_words
         for j in range(1, PACK):
             nc.sync.dma_start(out=planes[j][:], in_=x_rows[:, j, :])
         w_rows = w1.rearrange("(p j) c -> p j c", j=PACK)
-        w_raw = [keep.tile([P, PACK, H // 4], F32, name="w_raw%d" % c, tag="w_raw%d" % c, align_bytes=64) for c in range(4)]
-        for c in range(4):
-            nc.sync.dma_start(out=w_raw[c][:], in_=w_rows[:, :, c * (H // 4) : (c + 1) * (H // 4)])
+        chunk = H // W_CHUNKS
+        w_raw = [keep.tile([P, PACK, chunk], F32, name="w_raw%d" % c, tag="w_raw%d" % c, align_bytes=64) for c in range(W_CHUNKS)]
+        for c in range(W_CHUNKS):
+            nc.sync.dma_start(out=w_raw[c][:], in_=w_rows[:, :, c * chunk : (c + 1) * chunk])
 
         tail_words = []
         tail_scales = []
-        for i, (words, scales) in enumerate(((w2_words, w2_scales), (w3_words, w3_scales))):
-            wt = keep.tile([P, N], I32, name="tail_words%d" % i, align_bytes=64)
-            nc.sync.dma_start(out=wt[:], in_=words[0].rearrange("p n t -> p (n t)").bitcast(I32))
-            tail_words.append(wt)
-        for i, (words, scales) in enumerate(((w2_words, w2_scales), (w3_words, w3_scales))):
-            st = keep.tile([P, N], U8, name="tail_scales%d" % i, align_bytes=64)
-            nc.gpsimd.memset(st[:], 0)
-            for q in range(4):
-                nc.sync.dma_start(out=st[32 * q : 32 * q + 4, :].bitcast(I32), in_=scales[0, 4 * q : 4 * q + 4, :].bitcast(I32))
-            tail_scales.append(st)
+        for i, words in enumerate((w2_words, w3_words)):
+            word_tile = keep.tile([P, N], I32, name="tail_words%d" % i, align_bytes=64)
+            nc.sync.dma_start(out=word_tile[:], in_=words[0].rearrange("p n t -> p (n t)").bitcast(I32))
+            tail_words.append(word_tile)
+        for i, scale_rows in enumerate((w2_scales, w3_scales)):
+            scale_tile = keep.tile([P, N], U8, name="tail_scales%d" % i, align_bytes=64)
+            nc.gpsimd.memset(scale_tile[:], 0)
+            for r in range(QUADRANTS):
+                nc.sync.dma_start(
+                    out=scale_tile[32 * r : 32 * r + 4, :].bitcast(I32), in_=scale_rows[0, 4 * r : 4 * r + 4, :].bitcast(I32)
+                )
+            tail_scales.append(scale_tile)
 
         warm = keep.tile([P, 2], F32, name="warm")
-        nc.gpsimd.memset(warm[:, 0:1], 1.0)
+        nc.vector.memset(warm[:, 0:1], 1.0)
         nc.scalar.activation(out=warm[:, 1:2], in_=warm[:, 0:1], func=ACT.Sqrt)
 
         stage = keep.tile([P, 3, D * VH * PACK], BF16, name="stage", align_bytes=64)
         picked = stage[:, 0:3:2, :].rearrange("p h (d v j) -> p h d v j", d=D, j=PACK)
         w_grouped = stage[:, 1, :].rearrange("p (t m j) -> p t m j", t=PACK, j=PACK)
-        for j in range(PACK - 1):
+
+        last_plane = PACK - 1
+        pair_columns = S // 16 // 2
+        for j in range(last_plane):
             nc.vector.tensor_copy(out=picked[:, :, :, :, j].rearrange("p h d v -> p d h v"), in_=planes[j][:].indirect(offsets[:]))
         nc.vector.tensor_copy(
-            out=picked[:, :, 0:2, :, PACK - 1].rearrange("p h d v -> p d h v"),
-            in_=planes[PACK - 1][:].indirect(offsets[:, 0:32]),
+            out=picked[:, :, 0:2, :, last_plane].rearrange("p h d v -> p d h v"),
+            in_=planes[last_plane][:].indirect(offsets[:, :pair_columns]),
         )
-        last = keep.tile([P, 2, 2, VH], BF16, name="last", align_bytes=64)
-        nc.vector.tensor_copy(out=last[:].rearrange("p d h v -> p (d h v)"), in_=planes[PACK - 1][:].indirect(offsets[:, 32:64]))
+        late_cd = keep.tile([P, 2, 2, VH], BF16, name="late_cd", align_bytes=64)
+        nc.vector.tensor_copy(
+            out=late_cd[:].rearrange("p d h v -> p (d h v)"), in_=planes[last_plane][:].indirect(offsets[:, pair_columns:])
+        )
 
-        def cast(c, slots):
+        def round_w(c, slices):
             nc.scalar.copy(
-                out=w_grouped[:, slots, c * (P // 4) : (c + 1) * (P // 4), :].rearrange("p t m j -> p m j t"),
-                in_=w_raw[c][:].rearrange("p j (m t) -> p m j t", t=PACK)[:, :, :, slots],
+                out=w_grouped[:, slices, c * chunk // PACK : (c + 1) * chunk // PACK, :].rearrange("p t m j -> p m j t"),
+                in_=w_raw[c][:].rearrange("p j (m t) -> p m j t", t=PACK)[:, :, :, slices],
             )
 
-        for c in range(3):
-            cast(c, slice(0, PACK))
-        cast(3, slice(0, 2))
-        cast(3, slice(2, PACK))
+        for c in range(W_CHUNKS - 1):
+            round_w(c, slice(0, PACK))
+        round_w(W_CHUNKS - 1, slice(0, 2))
+        round_w(W_CHUNKS - 1, slice(2, PACK))
 
-        def quantize(src, width, name, tag=""):
+        def mx_tiles(width, name, tag=""):
             codes = keep.tile([P, width], U32, name=name + "_codes", tag=tag, align_bytes=64)
             scales = keep.tile([P, width], U8, name=name + "_scales", align_bytes=64)
+            return codes, scales
+
+        def quantize(src, width, name, tag=""):
+            codes, scales = mx_tiles(width, name, tag)
             nc.vector.quantize_mx(out=codes[:].bitcast(FP8X4), scales=scales[:], in_=src)
             return codes, scales
 
         x_ab0 = quantize(picked[:, 0, 0:2].rearrange("p d v j -> p (d v j)"), 2 * VH, "x_ab0")
         w_q = [quantize(w_grouped[:, t].rearrange("p m j -> p (m j)"), P, "w%d" % t) for t in range(PACK)]
-        for d in range(2):
-            nc.vector.tensor_copy(out=picked[:, :, 2 + d, :, PACK - 1], in_=last[:, d])
+        for n in range(2):
+            nc.vector.tensor_copy(out=picked[:, :, 2 + n, :, last_plane], in_=late_cd[:, n])
         x_c0 = quantize(picked[:, 0, 2].rearrange("p v j -> p (v j)"), VH, "x_c0")
-        x_ab1 = quantize(picked[:, 1, 0:2].rearrange("p d v j -> p (d v j)"), 2 * VH, "x_ab1", tag="w_raw3")
+        x_ab1 = quantize(picked[:, 1, 0:2].rearrange("p d v j -> p (d v j)"), 2 * VH, "x_ab1", tag="w_raw%d" % (W_CHUNKS - 1))
         x_d0 = quantize(picked[:, 0, 3].rearrange("p v j -> p (v j)"), VH, "x_d0")
         x_cd1 = quantize(picked[:, 1, 2:4].rearrange("p d v j -> p (d v j)"), 2 * VH, "x_cd1")
 
-        def moving(d, vh):
-            if vh == 0 and d >= 2:
-                (codes, scales), at = (x_c0, x_d0)[d - 2], 0
-            else:
-                (codes, scales), at = ((x_ab0, None), (x_ab1, x_cd1))[vh][d // 2], d % 2
-            cols = slice(at * VH, (at + 1) * VH)
-            return codes[:, cols].bitcast(FP8X4), scales[:, cols]
+        x_q = (
+            ((x_ab0, 0), (x_ab0, 1), (x_c0, 0), (x_d0, 0)),
+            ((x_ab1, 0), (x_ab1, 1), (x_cd1, 0), (x_cd1, 1)),
+        )
 
-        def product(bank, pieces, vh):
+        def product(dst, pieces, half):
             for t in range(PACK):
-                for n, d in enumerate(pieces):
-                    rhs, rhs_scale = moving(d, vh)
+                for n, piece in enumerate(pieces):
+                    (codes, scales), place = x_q[half][piece]
+                    cols = slice(place * VH, (place + 1) * VH)
                     nc.tensor.matmul_mx(
-                        out=bank[:, t, :],
+                        out=dst[:, t, :],
                         lhsT=w_q[t][0][:].bitcast(FP8X4),
                         lhsT_scale=w_q[t][1][:],
-                        rhs=rhs,
-                        rhs_scale=rhs_scale,
+                        rhs=codes[:, cols].bitcast(FP8X4),
+                        rhs_scale=scales[:, cols],
                         start=(n == 0),
                         stop=(n == len(pieces) - 1),
                     )
 
-        def woven(bank):
-            return bank[:].rearrange("p t v -> p v t")
+        def woven(src):
+            return src[:].rearrange("p t v -> p v t")
 
-        def work(name, tag=""):
-            return keep.tile([P, VH, PACK], F32, name=name, tag=tag, align_bytes=64)
+        def work(name, tag="", width=VH):
+            return keep.tile([P, width, PACK], F32, name=name, tag=tag, align_bytes=64)
 
         def bank(name, tag=""):
             return psum.tile([P, PACK, VH], F32, name=name, tag=tag)
 
-        def stt(dst, src, factor, other, op1=ALU.add):
+        def combine(dst, src, factor, other, op1=ALU.add):
             nc.vector.scalar_tensor_tensor(out=dst, in0=woven(src), scalar=factor, in1=other[:], op0=ALU.mult, op1=op1)
 
-        bank_u = [bank("bank_u%d" % vh) for vh in range(2)]
-        bank_a = [bank("bank_a%d" % vh, "a%d" % vh) for vh in range(2)]
-        bank_c = [bank("bank_c%d" % vh) for vh in range(2)]
-        bank_d = [bank("bank_d%d" % vh) for vh in range(2)]
-        u4 = [work("u4_%d" % vh) for vh in range(2)]
+        bank_u = [bank("bank_u%d" % half) for half in range(2)]
+        bank_a = [bank("bank_a%d" % half, "a%d" % half) for half in range(2)]
+        bank_c = [bank("bank_c%d" % half) for half in range(2)]
+        bank_d = [bank("bank_d%d" % half) for half in range(2)]
+        u4 = [work("u4_%d" % half) for half in range(2)]
 
         product(bank_u[0], (0, 1), 0)
         nc.scalar.activation(out=u4[0][:], in_=woven(bank_u[0]), func=ACT.Copy, scale=0.25)
@@ -146,70 +162,56 @@ def tile_picked_statpool_none_e_kernel(tc, xT, w1, w2_words, w2_scales, w3_words
         product(bank_a[1], (0,), 1)
         product(bank_d[1], (3,), 1)
 
-        w4, sp, s2, s3 = [], [], [], []
-        q = [work("q%d" % vh) for vh in range(2)]
-        for vh in range(2):
-            pd = work("pd_%d" % vh)
-            stt(pd[:], bank_a[vh], 0.5, u4[vh], ALU.subtract)
-            sp.append(work("sp_%d" % vh))
-            nc.scalar.activation(out=sp[vh][:], in_=pd[:], func=ACT.Square, scale=math.sqrt(6.0))
-            w4.append(work("w4_%d" % vh))
-            stt(w4[vh][:], bank_c[vh], 0.25, u4[vh])
-            h2 = work("h2_%d" % vh)
-            stt(h2[:], bank_c[vh], -0.5, u4[vh])
-            s2.append(work("s2_%d" % vh))
-            nc.scalar.activation(out=s2[vh][:], in_=h2[:], func=ACT.Square, scale=math.sqrt(2.0))
-            h3 = work("h3_%d" % vh, "h3_%d" % vh)
-            stt(h3[:], bank_d[vh], -0.75, w4[vh])
-            if vh == 1:
-                s3_last = [keep.tile([P, VH // 2, PACK], F32, name="s3_1_%d" % c, tag="s3_1_%d" % c, align_bytes=64) for c in range(2)]
-                for c in range(2):
-                    nc.scalar.activation(out=s3_last[c][:], in_=h3[:, c * VH // 2 : (c + 1) * VH // 2], func=ACT.Square)
-            if vh == 0:
-                s3.append(work("s3_0"))
-                nc.scalar.activation(out=s3[0][:], in_=h3[:], func=ACT.Square)
-                t12 = work("t12_0")
-                nc.gpsimd.tensor_tensor(out=t12[:], in0=sp[0][:], in1=s2[0][:], op=ALU.add)
-                first_parts = (slice(0, 3 * VH // 4), slice(3 * VH // 4, VH))
-                for cols in first_parts:
-                    nc.gpsimd.tensor_tensor(out=q[0][:, cols], in0=t12[:, cols], in1=s3[0][:, cols], op=ALU.add)
+        total = [work("total%d" % half) for half in range(2)]
+
+        def contrasts(half):
+            ab = work("ab_%d" % half)
+            combine(ab[:], bank_a[half], 0.5, u4[half], ALU.subtract)
+            ab_sq = work("ab_sq_%d" % half)
+            nc.scalar.activation(out=ab_sq[:], in_=ab[:], func=ACT.Square, scale=math.sqrt(6.0))
+            three = work("three_%d" % half)
+            combine(three[:], bank_c[half], 0.25, u4[half])
+            uc = work("uc_%d" % half)
+            combine(uc[:], bank_c[half], -0.5, u4[half])
+            uc_sq = work("uc_sq_%d" % half)
+            nc.scalar.activation(out=uc_sq[:], in_=uc[:], func=ACT.Square, scale=math.sqrt(2.0))
+            ucd = work("ucd_%d" % half, "ucd_%d" % half)
+            combine(ucd[:], bank_d[half], -0.75, three)
+            return three, ab_sq, uc_sq, ucd
+
+        three0, ab_sq0, uc_sq0, ucd0 = contrasts(0)
+        ucd_sq0 = work("ucd_sq_0")
+        nc.scalar.activation(out=ucd_sq0[:], in_=ucd0[:], func=ACT.Square)
+        two0 = work("two_0")
+        nc.gpsimd.tensor_tensor(out=two0[:], in0=ab_sq0[:], in1=uc_sq0[:], op=ALU.add)
+        uneven = (slice(0, 3 * VH // 4), slice(3 * VH // 4, VH))
+        for cols in uneven:
+            nc.gpsimd.tensor_tensor(out=total[0][:, cols], in0=two0[:, cols], in1=ucd_sq0[:, cols], op=ALU.add)
+
+        three1, ab_sq1, uc_sq1, ucd1 = contrasts(1)
+        ucd_sq1 = [work("ucd_sq_1_%d" % c, "ucd_sq_1_%d" % c, VH // 2) for c in range(2)]
+        for c, cols in enumerate(parts(2)):
+            nc.scalar.activation(out=ucd_sq1[c][:], in_=ucd1[:, cols], func=ACT.Square)
 
         mean_b = keep.tile([P, 2, VH, PACK], BF16, name="mean_b", align_bytes=64)
-        for vh in range(2):
-            stt(mean_b[:, vh], bank_d[vh], 0.25, w4[vh])
-        t12 = work("t12_1", "t12_1")
-        for c in range(2):
-            cols = slice(c * VH // 2, (c + 1) * VH // 2)
-            nc.vector.tensor_tensor(out=t12[:, cols], in0=sp[1][:, cols], in1=s2[1][:, cols], op=ALU.add)
+        for half, three in enumerate((three0, three1)):
+            combine(mean_b[:, half], bank_d[half], 0.25, three)
+        two1 = work("two_1", "two_1")
+        for cols in parts(2):
+            nc.vector.tensor_tensor(out=two1[:, cols], in0=ab_sq1[:, cols], in1=uc_sq1[:, cols], op=ALU.add)
         dev_b = [
-            keep.tile([P, VH, PACK], BF16, name="dev_b0", tag="h3_1", align_bytes=64),
+            keep.tile([P, VH, PACK], BF16, name="dev_b0", tag="ucd_1", align_bytes=64),
             keep.tile([P, VH, PACK], BF16, name="dev_b1", align_bytes=64),
         ]
-        for cols in first_parts:
-            nc.scalar.activation(out=dev_b[0][:, cols], in_=q[0][:, cols], func=ACT.Sqrt, scale=1.0 / 3.0)
-        for c in range(4):
-            cols = slice(c * VH // 4, (c + 1) * VH // 4)
-            part = slice(c % 2 * VH // 4, (c % 2 + 1) * VH // 4)
-            nc.vector.tensor_tensor(out=q[1][:, cols], in0=t12[:, cols], in1=s3_last[c // 2][:, part], op=ALU.add)
-            nc.scalar.activation(out=dev_b[1][:, cols], in_=q[1][:, cols], func=ACT.Sqrt, scale=1.0 / 3.0)
-        mean_q = quantize(mean_b[:].rearrange("p h v t -> p (h v t)"), 2 * VH, "mean", tag="s3_1_0")
-        for vh in range(2):
-            if vh == 0:
-                dev_q = quantize(dev_b[vh][:].rearrange("p v t -> p (v t)"), VH, "dev0", tag="t12_1")
-            else:
-                dev_q = (
-                    keep.tile([P, VH], U32, name="dev1_codes", align_bytes=64),
-                    keep.tile([P, VH], U8, name="dev1_scales", align_bytes=64),
-                )
-                for c in range(2):
-                    part = slice(c * VH // 2, (c + 1) * VH // 2)
-                    nc.vector.quantize_mx(
-                        out=dev_q[0][:, part].bitcast(FP8X4),
-                        scales=dev_q[1][:, part],
-                        in_=dev_b[1][:, part].rearrange("p v t -> p (v t)"),
-                    )
-            cols = slice(vh * VH, (vh + 1) * VH)
-            acc = psum.tile([P, VH], F32, name="acc%d" % vh, tag="a%d" % vh)
+        for cols in uneven:
+            nc.scalar.activation(out=dev_b[0][:, cols], in_=total[0][:, cols], func=ACT.Sqrt, scale=1.0 / 3.0)
+        for c, cols in enumerate(parts(4)):
+            nc.vector.tensor_tensor(out=total[1][:, cols], in0=two1[:, cols], in1=ucd_sq1[c // 2][:, parts(4)[c % 2]], op=ALU.add)
+            nc.scalar.activation(out=dev_b[1][:, cols], in_=total[1][:, cols], func=ACT.Sqrt, scale=1.0 / 3.0)
+
+        def finish(half, mean_q, dev_q):
+            cols = slice(half * VH, (half + 1) * VH)
+            acc = psum.tile([P, VH], F32, name="acc%d" % half, tag="a%d" % half)
             for i, (codes, scales) in enumerate(((mean_q[0][:, cols], mean_q[1][:, cols]), (dev_q[0][:], dev_q[1][:]))):
                 nc.tensor.matmul_mx(
                     out=acc[:],
@@ -220,6 +222,18 @@ def tile_picked_statpool_none_e_kernel(tc, xT, w1, w2_words, w2_scales, w3_words
                     start=(i == 0),
                     stop=(i == 1),
                 )
-            result = keep.tile([P, VH], F32, name="result%d" % vh)
+            result = keep.tile([P, VH], F32, name="result%d" % half)
             nc.scalar.copy(out=result[:], in_=acc[:])
             nc.sync.dma_start(out=out[:, cols], in_=result[:])
+
+        means_q = quantize(mean_b[:].rearrange("p h v t -> p (h v t)"), 2 * VH, "mean", tag="ucd_sq_1_0")
+        dev0_q = quantize(dev_b[0][:].rearrange("p v t -> p (v t)"), VH, "dev0", tag="two_1")
+        finish(0, means_q, dev0_q)
+        dev1_q = mx_tiles(VH, "dev1")
+        for cols in parts(2):
+            nc.vector.quantize_mx(
+                out=dev1_q[0][:, cols].bitcast(FP8X4),
+                scales=dev1_q[1][:, cols],
+                in_=dev_b[1][:, cols].rearrange("p v t -> p (v t)"),
+            )
+        finish(1, means_q, dev1_q)

@@ -56,15 +56,14 @@ def tile_picked_statpool_none_e_kernel(tc, xT, w1, w2_words, w2_scales, w3_words
         for i, scale_rows in enumerate((w2_scales, w3_scales)):
             scale_tile = keep.tile([P, N], U8, name="tail_scales%d" % i, align_bytes=64)
             nc.gpsimd.memset(scale_tile[:], 0)
+            if i == 0:
+                warm = keep.tile([P, 1], F32, name="warm")
+                nc.scalar.activation(out=warm[:], in_=scale_tile[:, 0:4].bitcast(F32), func=ACT.Sqrt)
             for r in range(QUADRANTS):
                 nc.sync.dma_start(
                     out=scale_tile[32 * r : 32 * r + 4, :].bitcast(I32), in_=scale_rows[0, 4 * r : 4 * r + 4, :].bitcast(I32)
                 )
             tail_scales.append(scale_tile)
-
-        warm = keep.tile([P, 2], F32, name="warm")
-        nc.vector.memset(warm[:, 0:1], 1.0)
-        nc.scalar.activation(out=warm[:, 1:2], in_=warm[:, 0:1], func=ACT.Sqrt)
 
         stage = keep.tile([P, 3, D * VH * PACK], BF16, name="stage", align_bytes=64)
         picked = stage[:, 0:3:2, :].rearrange("p h (d v j) -> p h d v j", d=D, j=PACK)

@@ -2,6 +2,7 @@ import math
 from contextlib import ExitStack
 
 import concourse.mybir as mybir
+from concourse.masks import make_identity
 
 K, T, S, V, H, N = 512, 4096, 1024, 256, 512, 128
 FLOPS = 2 * K * H * S + 2 * 2 * H * N * V
@@ -64,6 +65,8 @@ def tile_picked_statpool_none_e_kernel(tc, xT, w1, w2_words, w2_scales, w3_words
                     out=scale_tile[32 * r : 32 * r + 4, :].bitcast(I32), in_=scale_rows[0, 4 * r : 4 * r + 4, :].bitcast(I32)
                 )
             tail_scales.append(scale_tile)
+        identity = keep.tile([P, P], F32, name="identity")
+        make_identity(nc, identity[:])
 
         stage = keep.tile([P, 3, D * VH * PACK], BF16, name="stage", align_bytes=64)
         picked = stage[:, 0:3:2, :].rearrange("p h (d v j) -> p h d v j", d=D, j=PACK)
@@ -104,7 +107,13 @@ def tile_picked_statpool_none_e_kernel(tc, xT, w1, w2_words, w2_scales, w3_words
             return codes, scales
 
         x_ab0 = quantize(picked[:, 0, 0:2].rearrange("p d v j -> p (d v j)"), 2 * VH, "x_ab0")
-        w_q = [quantize(w_grouped[:, t].rearrange("p m j -> p (m j)"), P, "w%d" % t) for t in range(PACK)]
+        w_q = mx_tiles(H, "w")
+        for t in range(PACK):
+            nc.vector.quantize_mx(
+                out=w_q[0][:, t * P : (t + 1) * P].bitcast(FP8X4),
+                scales=w_q[1][:, t * P : (t + 1) * P],
+                in_=w_grouped[:, t].rearrange("p m j -> p (m j)"),
+            )
         for n in range(2):
             nc.vector.tensor_copy(out=picked[:, :, 2 + n, :, last_plane], in_=late_cd[:, n])
         x_c0 = quantize(picked[:, 0, 2].rearrange("p v j -> p (v j)"), VH, "x_c0")
@@ -124,13 +133,28 @@ def tile_picked_statpool_none_e_kernel(tc, xT, w1, w2_words, w2_scales, w3_words
                     cols = slice(place * VH, (place + 1) * VH)
                     nc.tensor.matmul_mx(
                         out=dst[:, t, :],
-                        lhsT=w_q[t][0][:].bitcast(FP8X4),
-                        lhsT_scale=w_q[t][1][:],
+                        lhsT=w_q[0][:, t * P : (t + 1) * P].bitcast(FP8X4),
+                        lhsT_scale=w_q[1][:, t * P : (t + 1) * P],
                         rhs=codes[:, cols].bitcast(FP8X4),
                         rhs_scale=scales[:, cols],
                         start=(n == 0),
                         stop=(n == len(pieces) - 1),
                     )
+
+        def product_turned(dst, pieces, slices=slice(0, PACK)):
+            cols = slice(slices.start * P, slices.stop * P)
+            for n, piece in enumerate(pieces):
+                (codes, scales), place = x_q[0][piece]
+                frames = slice(place * VH, (place + 1) * VH)
+                nc.tensor.matmul_mx(
+                    out=dst[:].rearrange("p t m -> p (t m)")[:, cols],
+                    lhsT=codes[:, frames].bitcast(FP8X4),
+                    lhsT_scale=scales[:, frames],
+                    rhs=w_q[0][:, cols].bitcast(FP8X4),
+                    rhs_scale=w_q[1][:, cols],
+                    start=(n == 0),
+                    stop=(n == len(pieces) - 1),
+                )
 
         def woven(src):
             return src[:].rearrange("p t v -> p v t")
@@ -144,73 +168,88 @@ def tile_picked_statpool_none_e_kernel(tc, xT, w1, w2_words, w2_scales, w3_words
         def combine(dst, src, factor, other, op1=ALU.add):
             nc.vector.scalar_tensor_tensor(out=dst, in0=woven(src), scalar=factor, in1=other[:], op0=ALU.mult, op1=op1)
 
-        bank_u = [bank("bank_u%d" % half) for half in range(2)]
+        bank_u = [bank("bank_u%d" % half, "u%d" % half) for half in range(2)]
         bank_a = [bank("bank_a%d" % half, "a%d" % half) for half in range(2)]
-        bank_c = [bank("bank_c%d" % half) for half in range(2)]
-        bank_d = [bank("bank_d%d" % half) for half in range(2)]
-        u4 = [work("u4_%d" % half) for half in range(2)]
+        bank_c = [bank("bank_c%d" % half, "c%d" % half) for half in range(2)]
+        bank_early = bank("bank_early", "d1")
+        bank_d = [bank("bank_d%d" % half, "d%d" % half) for half in range(2)]
+        def rows(name, tag=""):
+            return keep.tile([P, PACK, P], F32, name=name, tag=tag, align_bytes=64)
 
-        product(bank_u[0], (0, 1), 0)
-        nc.scalar.activation(out=u4[0][:], in_=woven(bank_u[0]), func=ACT.Copy, scale=0.25)
-        product(bank_a[0], (0,), 0)
-        product(bank_c[0], (2,), 0)
+        u0 = rows("u0")
+        u1 = work("u1")
+        for src, pair in ((bank_early, slice(0, 2)), (bank_u[0], slice(2, 4))):
+            product_turned(src, (0, 1), pair)
+            nc.scalar.activation(out=u0[:, pair], in_=src[:, pair], func=ACT.Copy, scale=4.0 / 3.0)
+        product_turned(bank_a[0], (0,))
+        product_turned(bank_c[0], (2,))
         product(bank_u[1], (0, 1), 1)
-        nc.scalar.activation(out=u4[1][:], in_=woven(bank_u[1]), func=ACT.Copy, scale=0.25)
-        product(bank_d[0], (3,), 0)
-        product(bank_c[1], (2,), 1)
+        nc.scalar.activation(out=u1[:], in_=woven(bank_u[1]), func=ACT.Copy, scale=0.25)
+        product_turned(bank_d[0], (3,))
         product(bank_a[1], (0,), 1)
+        product(bank_c[1], (2,), 1)
         product(bank_d[1], (3,), 1)
 
-        total = [work("total%d" % half) for half in range(2)]
+        def from_bank(name, src, factor, other, op1):
+            dst = rows(name)
+            nc.vector.scalar_tensor_tensor(out=dst[:], in0=src[:], scalar=factor, in1=other[:], op0=ALU.mult, op1=op1)
+            return dst
 
-        def contrasts(half):
-            ab = work("ab_%d" % half)
-            combine(ab[:], bank_a[half], 0.5, u4[half], ALU.subtract)
-            ab_sq = work("ab_sq_%d" % half)
-            nc.scalar.activation(out=ab_sq[:], in_=ab[:], func=ACT.Square, scale=math.sqrt(6.0))
-            three = work("three_%d" % half)
-            combine(three[:], bank_c[half], 0.25, u4[half])
-            uc = work("uc_%d" % half)
-            combine(uc[:], bank_c[half], -0.5, u4[half])
-            uc_sq = work("uc_sq_%d" % half)
-            nc.scalar.activation(out=uc_sq[:], in_=uc[:], func=ACT.Square, scale=math.sqrt(2.0))
-            ucd = work("ucd_%d" % half, "ucd_%d" % half)
-            combine(ucd[:], bank_d[half], -0.75, three)
-            return three, ab_sq, uc_sq, ucd
+        def turn(dst, src, opens=False, closes=False):
+            for t in range(PACK):
+                nc.tensor.matmul(
+                    dst[:, t, :], lhsT=src[:, t, :], rhs=identity[:], is_transpose=True,
+                    start=(opens and t == 0), stop=(closes and t == PACK - 1),
+                )
 
-        three0, ab_sq0, uc_sq0, ucd0 = contrasts(0)
-        ucd_sq0 = work("ucd_sq_0")
-        nc.scalar.activation(out=ucd_sq0[:], in_=ucd0[:], func=ACT.Square)
-        two0 = work("two_0")
-        nc.gpsimd.tensor_tensor(out=two0[:], in0=ab_sq0[:], in1=uc_sq0[:], op=ALU.add)
-        uneven = (slice(0, 3 * VH // 4), slice(3 * VH // 4, VH))
-        for cols in uneven:
-            nc.gpsimd.tensor_tensor(out=total[0][:, cols], in0=two0[:, cols], in1=ucd_sq0[:, cols], op=ALU.add)
+        ab0 = from_bank("ab0", bank_a[0], 8.0 / 3.0, u0, ALU.subtract)
+        three0 = from_bank("three0", bank_c[0], 4.0 / 3.0, u0, ALU.add)
+        uc0 = from_bank("uc0", bank_c[0], 8.0 / 3.0, u0, ALU.subtract)
+        ucd0 = rows("ucd0")
+        nc.vector.scalar_tensor_tensor(out=ucd0[:], in0=three0[:], scalar=-0.25, in1=bank_d[0][:], op0=ALU.mult, op1=ALU.add)
+        ab_sq0, uc_sq0, ucd_sq0 = rows("ab_sq0"), rows("uc_sq0"), rows("ucd_sq0")
+        nc.gpsimd.tensor_tensor(out=ab_sq0[:], in0=ab0[:], in1=ab0[:], op=ALU.mult)
+        nc.scalar.activation(out=uc_sq0[:], in_=uc0[:], func=ACT.Square, scale=math.sqrt(1.0 / 3.0))
+        nc.scalar.activation(out=ucd_sq0[:], in_=ucd0[:], func=ACT.Square, scale=math.sqrt(8.0 / 3.0))
+        var0 = bank("var0", "u0")
+        sum0 = bank("sum0", "a0")
+        turn(sum0, three0, opens=True)
+        turn(var0, ab_sq0, opens=True)
+        turn(sum0, ucd0, closes=True)
+        turn(var0, uc_sq0)
+        turn(var0, ucd_sq0, closes=True)
 
-        three1, ab_sq1, uc_sq1, ucd1 = contrasts(1)
+        ab1, uc1, three1, ucd1 = work("ab1"), work("uc1"), work("three1"), work("ucd1")
+        ab_sq1, uc_sq1 = work("ab_sq1"), work("uc_sq1", "uc_sq1")
+        combine(ab1[:], bank_a[1], 0.5, u1, ALU.subtract)
+        nc.scalar.activation(out=ab_sq1[:], in_=ab1[:], func=ACT.Square, scale=math.sqrt(6.0))
+        combine(three1[:], bank_c[1], 0.25, u1)
+        combine(uc1[:], bank_c[1], -0.5, u1)
+        nc.scalar.activation(out=uc_sq1[:], in_=uc1[:], func=ACT.Square, scale=math.sqrt(2.0))
+        combine(ucd1[:], bank_d[1], -0.75, three1)
+        mean_b = keep.tile([P, 2, VH, PACK], BF16, name="mean_b", align_bytes=64)
+        nc.scalar.activation(out=mean_b[:, 0], in_=woven(sum0), func=ACT.Copy, scale=0.25)
         ucd_sq1 = [work("ucd_sq_1_%d" % c, "ucd_sq_1_%d" % c, VH // 2) for c in range(2)]
         for c, cols in enumerate(parts(2)):
             nc.scalar.activation(out=ucd_sq1[c][:], in_=ucd1[:, cols], func=ACT.Square)
 
-        mean_b = keep.tile([P, 2, VH, PACK], BF16, name="mean_b", align_bytes=64)
-        for half, three in enumerate((three0, three1)):
-            combine(mean_b[:, half], bank_d[half], 0.25, three)
+        combine(mean_b[:, 1], bank_d[1], 0.25, three1)
         two1 = work("two_1", "two_1")
         for cols in parts(2):
             nc.vector.tensor_tensor(out=two1[:, cols], in0=ab_sq1[:, cols], in1=uc_sq1[:, cols], op=ALU.add)
         dev_b = [
-            keep.tile([P, VH, PACK], BF16, name="dev_b0", tag="ucd_1", align_bytes=64),
+            keep.tile([P, VH, PACK], BF16, name="dev_b0", align_bytes=64),
             keep.tile([P, VH, PACK], BF16, name="dev_b1", align_bytes=64),
         ]
-        for cols in uneven:
-            nc.scalar.activation(out=dev_b[0][:, cols], in_=total[0][:, cols], func=ACT.Sqrt, scale=1.0 / 3.0)
+        nc.scalar.activation(out=dev_b[0][:], in_=woven(var0), func=ACT.Sqrt, scale=9.0 / 128.0)
+        total1 = work("total1")
         for c, cols in enumerate(parts(4)):
-            nc.vector.tensor_tensor(out=total[1][:, cols], in0=two1[:, cols], in1=ucd_sq1[c // 2][:, parts(4)[c % 2]], op=ALU.add)
-            nc.scalar.activation(out=dev_b[1][:, cols], in_=total[1][:, cols], func=ACT.Sqrt, scale=1.0 / 3.0)
+            nc.vector.tensor_tensor(out=total1[:, cols], in0=two1[:, cols], in1=ucd_sq1[c // 2][:, parts(4)[c % 2]], op=ALU.add)
+            nc.scalar.activation(out=dev_b[1][:, cols], in_=total1[:, cols], func=ACT.Sqrt, scale=1.0 / 3.0)
 
         def finish(half, mean_q, dev_q):
             cols = slice(half * VH, (half + 1) * VH)
-            acc = psum.tile([P, VH], F32, name="acc%d" % half, tag="a%d" % half)
+            acc = psum.tile([P, VH], F32, name="acc%d" % half, tag="c%d" % half)
             for i, (codes, scales) in enumerate(((mean_q[0][:, cols], mean_q[1][:, cols]), (dev_q[0][:], dev_q[1][:]))):
                 nc.tensor.matmul_mx(
                     out=acc[:],

@@ -68,9 +68,9 @@ def tile_picked_statpool_none_e_kernel(tc, xT, w1, w2_words, w2_scales, w3_words
         identity = keep.tile([P, P], F32, name="identity")
         make_identity(nc, identity[:])
 
-        stage = keep.tile([P, 3, D * VH * PACK], BF16, name="stage", align_bytes=64)
-        picked = stage[:, 0:3:2, :].rearrange("p h (d v j) -> p h d v j", d=D, j=PACK)
-        w_grouped = stage[:, 1, :].rearrange("p (t m j) -> p t m j", t=PACK, j=PACK)
+        stage = keep.tile([P, 4, D * VH * PACK], BF16, name="stage", align_bytes=64)
+        picked = stage[:, 0:4:2, :].rearrange("p h (d v j) -> p h d v j", d=D, j=PACK)
+        w_grouped = stage[:, 1:4:2, : 2 * P * PACK].rearrange("p a (b m j) -> p a b m j", b=2, j=PACK)
 
         last_plane = PACK - 1
         pair_columns = S // 16 // 2
@@ -85,16 +85,16 @@ def tile_picked_statpool_none_e_kernel(tc, xT, w1, w2_words, w2_scales, w3_words
             out=late_cd[:].rearrange("p d h v -> p (d h v)"), in_=planes[last_plane][:].indirect(offsets[:, pair_columns:])
         )
 
-        def round_w(c, slices):
+        def round_w(c, pairs):
             nc.scalar.copy(
-                out=w_grouped[:, slices, c * chunk // PACK : (c + 1) * chunk // PACK, :].rearrange("p t m j -> p m j t"),
-                in_=w_raw[c][:].rearrange("p j (m t) -> p m j t", t=PACK)[:, :, :, slices],
+                out=w_grouped[:, pairs, :, c * chunk // PACK : (c + 1) * chunk // PACK, :].rearrange("p a b m j -> p m j a b"),
+                in_=w_raw[c][:].rearrange("p j (m a b) -> p m j a b", a=2, b=2)[:, :, :, pairs],
             )
 
         for c in range(W_CHUNKS - 1):
-            round_w(c, slice(0, PACK))
-        round_w(W_CHUNKS - 1, slice(0, 2))
-        round_w(W_CHUNKS - 1, slice(2, PACK))
+            round_w(c, slice(0, 2))
+        round_w(W_CHUNKS - 1, slice(0, 1))
+        round_w(W_CHUNKS - 1, slice(1, 2))
 
         def mx_tiles(width, name, tag=""):
             codes = keep.tile([P, width], U32, name=name + "_codes", tag=tag, align_bytes=64)
@@ -112,10 +112,10 @@ def tile_picked_statpool_none_e_kernel(tc, xT, w1, w2_words, w2_scales, w3_words
             nc.vector.quantize_mx(
                 out=w_q[0][:, t * P : (t + 1) * P].bitcast(FP8X4),
                 scales=w_q[1][:, t * P : (t + 1) * P],
-                in_=w_grouped[:, t].rearrange("p m j -> p (m j)"),
+                in_=w_grouped[:, t // 2, t % 2].rearrange("p m j -> p (m j)"),
             )
-        for n in range(2):
-            nc.vector.tensor_copy(out=picked[:, :, 2 + n, :, last_plane], in_=late_cd[:, n])
+        for n, copy in enumerate((nc.vector.tensor_copy, nc.scalar.copy)):
+            copy(out=picked[:, :, 2 + n, :, last_plane], in_=late_cd[:, n])
         x_c0 = quantize(picked[:, 0, 2].rearrange("p v j -> p (v j)"), VH, "x_c0")
         x_ab1 = quantize(picked[:, 1, 0:2].rearrange("p d v j -> p (d v j)"), 2 * VH, "x_ab1", tag="w_raw%d" % (W_CHUNKS - 1))
         x_d0 = quantize(picked[:, 0, 3].rearrange("p v j -> p (v j)"), VH, "x_d0")
@@ -179,7 +179,8 @@ def tile_picked_statpool_none_e_kernel(tc, xT, w1, w2_words, w2_scales, w3_words
         u0 = rows("u0")
         u1 = work("u1")
         for src, pair in ((bank_early, slice(0, 2)), (bank_u[0], slice(2, 4))):
-            product_turned(src, (0, 1), pair)
+            for t in range(pair.start, pair.stop):
+                product_turned(src, (0, 1), slice(t, t + 1))
             nc.scalar.activation(out=u0[:, pair], in_=src[:, pair], func=ACT.Copy, scale=4.0 / 3.0)
         product_turned(bank_a[0], (0,))
         product_turned(bank_c[0], (2,))
@@ -223,10 +224,13 @@ def tile_picked_statpool_none_e_kernel(tc, xT, w1, w2_words, w2_scales, w3_words
         ab_sq1, uc_sq1 = work("ab_sq1"), work("uc_sq1", "uc_sq1")
         combine(ab1[:], bank_a[1], 0.5, u1, ALU.subtract)
         nc.scalar.activation(out=ab_sq1[:], in_=ab1[:], func=ACT.Square, scale=math.sqrt(6.0))
-        combine(three1[:], bank_c[1], 0.25, u1)
         combine(uc1[:], bank_c[1], -0.5, u1)
         nc.scalar.activation(out=uc_sq1[:], in_=uc1[:], func=ACT.Square, scale=math.sqrt(2.0))
-        combine(ucd1[:], bank_d[1], -0.75, three1)
+        for dst, src, factor, other in ((three1, bank_c[1], 0.25, u1), (ucd1, bank_d[1], -0.75, three1)):
+            for cols in parts(2):
+                nc.vector.scalar_tensor_tensor(
+                    out=dst[:, cols], in0=woven(src)[:, cols], scalar=factor, in1=other[:, cols], op0=ALU.mult, op1=ALU.add
+                )
         mean_b = keep.tile([P, 2, VH, PACK], BF16, name="mean_b", align_bytes=64)
         nc.scalar.activation(out=mean_b[:, 0], in_=woven(sum0), func=ACT.Copy, scale=0.25)
         ucd_sq1 = [work("ucd_sq_1_%d" % c, "ucd_sq_1_%d" % c, VH // 2) for c in range(2)]
@@ -235,8 +239,8 @@ def tile_picked_statpool_none_e_kernel(tc, xT, w1, w2_words, w2_scales, w3_words
 
         combine(mean_b[:, 1], bank_d[1], 0.25, three1)
         two1 = work("two_1", "two_1")
-        for cols in parts(2):
-            nc.vector.tensor_tensor(out=two1[:, cols], in0=ab_sq1[:, cols], in1=uc_sq1[:, cols], op=ALU.add)
+        for engine, cols in zip((nc.gpsimd, nc.vector), (slice(0, 3 * VH // 4), slice(3 * VH // 4, VH))):
+            engine.tensor_tensor(out=two1[:, cols], in0=ab_sq1[:, cols], in1=uc_sq1[:, cols], op=ALU.add)
         dev_b = [
             keep.tile([P, VH, PACK], BF16, name="dev_b0", align_bytes=64),
             keep.tile([P, VH, PACK], BF16, name="dev_b1", align_bytes=64),

@@ -68,33 +68,33 @@ def tile_picked_statpool_none_e_kernel(tc, xT, w1, w2_words, w2_scales, w3_words
         identity = keep.tile([P, P], F32, name="identity")
         make_identity(nc, identity[:])
 
-        stage = keep.tile([P, 4, D * VH * PACK], BF16, name="stage", align_bytes=64)
+        stage = keep.tile([P, 8, D * VH * PACK], BF16, name="stage", align_bytes=64)
         picked = stage[:, 0:4:2, :].rearrange("p h (d v j) -> p h d v j", d=D, j=PACK)
-        w_grouped = stage[:, 1:4:2, : 2 * P * PACK].rearrange("p a (b m j) -> p a b m j", b=2, j=PACK)
+        w_grouped = stage[:, 1:8:2, : P * PACK].rearrange("p t (m j) -> p t m j", j=PACK)
 
         last_plane = PACK - 1
-        pair_columns = S // 16 // 2
+        pair_columns = 3 * S // 16 // D
         for j in range(last_plane):
             nc.vector.tensor_copy(out=picked[:, :, :, :, j].rearrange("p h d v -> p d h v"), in_=planes[j][:].indirect(offsets[:]))
         nc.vector.tensor_copy(
-            out=picked[:, :, 0:2, :, last_plane].rearrange("p h d v -> p d h v"),
+            out=picked[:, :, 0:3, :, last_plane].rearrange("p h d v -> p d h v"),
             in_=planes[last_plane][:].indirect(offsets[:, :pair_columns]),
         )
-        late_cd = keep.tile([P, 2, 2, VH], BF16, name="late_cd", align_bytes=64)
+        late_cd = keep.tile([P, 2, VH], BF16, name="late_cd", align_bytes=64)
         nc.vector.tensor_copy(
-            out=late_cd[:].rearrange("p d h v -> p (d h v)"), in_=planes[last_plane][:].indirect(offsets[:, pair_columns:])
+            out=late_cd[:].rearrange("p h v -> p (h v)"), in_=planes[last_plane][:].indirect(offsets[:, pair_columns:])
         )
 
-        def round_w(c, pairs):
+        def round_w(c, slices):
             nc.scalar.copy(
-                out=w_grouped[:, pairs, :, c * chunk // PACK : (c + 1) * chunk // PACK, :].rearrange("p a b m j -> p m j a b"),
-                in_=w_raw[c][:].rearrange("p j (m a b) -> p m j a b", a=2, b=2)[:, :, :, pairs],
+                out=w_grouped[:, slices, c * chunk // PACK : (c + 1) * chunk // PACK, :].rearrange("p t m j -> p m j t"),
+                in_=w_raw[c][:].rearrange("p j (m t) -> p m j t", t=PACK)[:, :, :, slices],
             )
 
         for c in range(W_CHUNKS - 1):
-            round_w(c, slice(0, 2))
-        round_w(W_CHUNKS - 1, slice(0, 1))
-        round_w(W_CHUNKS - 1, slice(1, 2))
+            round_w(c, slice(0, PACK))
+        round_w(W_CHUNKS - 1, slice(0, 2))
+        round_w(W_CHUNKS - 1, slice(2, PACK))
 
         def mx_tiles(width, name, tag=""):
             codes = keep.tile([P, width], U32, name=name + "_codes", tag=tag, align_bytes=64)
@@ -112,18 +112,24 @@ def tile_picked_statpool_none_e_kernel(tc, xT, w1, w2_words, w2_scales, w3_words
             nc.vector.quantize_mx(
                 out=w_q[0][:, t * P : (t + 1) * P].bitcast(FP8X4),
                 scales=w_q[1][:, t * P : (t + 1) * P],
-                in_=w_grouped[:, t // 2, t % 2].rearrange("p m j -> p (m j)"),
+                in_=w_grouped[:, t].rearrange("p m j -> p (m j)"),
             )
-        for n, copy in enumerate((nc.vector.tensor_copy, nc.scalar.copy)):
-            copy(out=picked[:, :, 2 + n, :, last_plane], in_=late_cd[:, n])
-        x_c0 = quantize(picked[:, 0, 2].rearrange("p v j -> p (v j)"), VH, "x_c0")
-        x_ab1 = quantize(picked[:, 1, 0:2].rearrange("p d v j -> p (d v j)"), 2 * VH, "x_ab1", tag="w_raw%d" % (W_CHUNKS - 1))
+        nc.scalar.copy(out=picked[:, :, 3, :, last_plane], in_=late_cd[:])
+        x_c0 = quantize(picked[:, 0, 2].rearrange("p v j -> p (v j)"), VH, "x_c0", tag="w_raw2")
+        x_abc1 = mx_tiles(3 * VH, "x_abc1", tag="w_raw%d" % (W_CHUNKS - 1))
+        for pieces in (slice(0, 2), slice(2, 3)):
+            cols = slice(pieces.start * VH, pieces.stop * VH)
+            nc.vector.quantize_mx(
+                out=x_abc1[0][:, cols].bitcast(FP8X4),
+                scales=x_abc1[1][:, cols],
+                in_=picked[:, 1, pieces].rearrange("p d v j -> p (d v j)"),
+            )
         x_d0 = quantize(picked[:, 0, 3].rearrange("p v j -> p (v j)"), VH, "x_d0")
-        x_cd1 = quantize(picked[:, 1, 2:4].rearrange("p d v j -> p (d v j)"), 2 * VH, "x_cd1")
+        x_d1 = quantize(picked[:, 1, 3].rearrange("p v j -> p (v j)"), VH, "x_d1")
 
         x_q = (
             ((x_ab0, 0), (x_ab0, 1), (x_c0, 0), (x_d0, 0)),
-            ((x_ab1, 0), (x_ab1, 1), (x_cd1, 0), (x_cd1, 1)),
+            ((x_abc1, 0), (x_abc1, 1), (x_abc1, 2), (x_d1, 0)),
         )
 
         def product(dst, pieces, half):
@@ -141,13 +147,15 @@ def tile_picked_statpool_none_e_kernel(tc, xT, w1, w2_words, w2_scales, w3_words
                         stop=(n == len(pieces) - 1),
                     )
 
-        def product_turned(dst, pieces, slices=slice(0, PACK)):
+        def product_turned(dst, pieces, slices=slice(0, PACK), place_in=None):
             cols = slice(slices.start * P, slices.stop * P)
+            place_in = place_in or slices
+            dst_cols = slice(place_in.start * P, place_in.stop * P)
             for n, piece in enumerate(pieces):
                 (codes, scales), place = x_q[0][piece]
                 frames = slice(place * VH, (place + 1) * VH)
                 nc.tensor.matmul_mx(
-                    out=dst[:].rearrange("p t m -> p (t m)")[:, cols],
+                    out=dst[:].rearrange("p t m -> p (t m)")[:, dst_cols],
                     lhsT=codes[:, frames].bitcast(FP8X4),
                     lhsT_scale=scales[:, frames],
                     rhs=w_q[0][:, cols].bitcast(FP8X4),
@@ -168,21 +176,20 @@ def tile_picked_statpool_none_e_kernel(tc, xT, w1, w2_words, w2_scales, w3_words
         def combine(dst, src, factor, other, op1=ALU.add):
             nc.vector.scalar_tensor_tensor(out=dst, in0=woven(src), scalar=factor, in1=other[:], op0=ALU.mult, op1=op1)
 
-        bank_u = [bank("bank_u%d" % half, "u%d" % half) for half in range(2)]
+        bank_u = [bank("bank_b0", "u0"), bank("bank_u1", "u1")]
         bank_a = [bank("bank_a%d" % half, "a%d" % half) for half in range(2)]
         bank_c = [bank("bank_c%d" % half, "c%d" % half) for half in range(2)]
-        bank_early = bank("bank_early", "d1")
         bank_d = [bank("bank_d%d" % half, "d%d" % half) for half in range(2)]
+
         def rows(name, tag=""):
             return keep.tile([P, PACK, P], F32, name=name, tag=tag, align_bytes=64)
 
-        u0 = rows("u0")
-        u1 = work("u1")
-        for src, pair in ((bank_early, slice(0, 2)), (bank_u[0], slice(2, 4))):
-            for t in range(pair.start, pair.stop):
-                product_turned(src, (0, 1), slice(t, t + 1))
-            nc.scalar.activation(out=u0[:, pair], in_=src[:, pair], func=ACT.Copy, scale=4.0 / 3.0)
-        product_turned(bank_a[0], (0,))
+        a0 = rows("a0", "sums")
+        u1 = work("u1", "late")
+        for t in range(PACK):
+            product_turned(bank_a[0], (0,), slice(t, t + 1))
+        nc.scalar.activation(out=a0[:], in_=bank_a[0][:], func=ACT.Copy, scale=4.0 / 3.0)
+        product_turned(bank_u[0], (1,))
         product_turned(bank_c[0], (2,))
         product(bank_u[1], (0, 1), 1)
         nc.scalar.activation(out=u1[:], in_=woven(bank_u[1]), func=ACT.Copy, scale=0.25)
@@ -192,7 +199,7 @@ def tile_picked_statpool_none_e_kernel(tc, xT, w1, w2_words, w2_scales, w3_words
         product(bank_d[1], (3,), 1)
 
         def from_bank(name, src, factor, other, op1):
-            dst = rows(name)
+            dst = rows(name, name)
             nc.vector.scalar_tensor_tensor(out=dst[:], in0=src[:], scalar=factor, in1=other[:], op0=ALU.mult, op1=op1)
             return dst
 
@@ -203,24 +210,31 @@ def tile_picked_statpool_none_e_kernel(tc, xT, w1, w2_words, w2_scales, w3_words
                     start=(opens and t == 0), stop=(closes and t == PACK - 1),
                 )
 
-        ab0 = from_bank("ab0", bank_a[0], 8.0 / 3.0, u0, ALU.subtract)
-        three0 = from_bank("three0", bank_c[0], 4.0 / 3.0, u0, ALU.add)
-        uc0 = from_bank("uc0", bank_c[0], 8.0 / 3.0, u0, ALU.subtract)
+        u0, three0 = rows("u0"), rows("three0")
+        for dst, src, other in ((u0, bank_u[0], a0), (three0, bank_c[0], u0)):
+            for pair in (slice(0, 2), slice(2, 4)):
+                nc.vector.scalar_tensor_tensor(
+                    out=dst[:, pair], in0=src[:, pair], scalar=4.0 / 3.0, in1=other[:, pair], op0=ALU.mult, op1=ALU.add
+                )
+        ab0 = from_bank("ab0", bank_u[0], 4.0 / 3.0, a0, ALU.subtract)
+        ab_sq0, uc_sq0, ucd_sq0 = rows("ab_sq0"), rows("uc_sq0"), rows("ucd_sq0")
+        nc.scalar.activation(out=ab_sq0[:], in_=ab0[:], func=ACT.Square, scale=math.sqrt(0.75))
+        u0_twice, uc0 = rows("u0_twice"), rows("uc0")
+        nc.gpsimd.tensor_scalar(out=u0_twice[:], in0=u0[:], scalar1=1.5, scalar2=0.0, op0=ALU.mult, op1=ALU.add)
+        nc.gpsimd.tensor_tensor(out=uc0[:], in0=three0[:], in1=u0_twice[:], op=ALU.subtract)
         ucd0 = rows("ucd0")
         nc.vector.scalar_tensor_tensor(out=ucd0[:], in0=three0[:], scalar=-0.25, in1=bank_d[0][:], op0=ALU.mult, op1=ALU.add)
-        ab_sq0, uc_sq0, ucd_sq0 = rows("ab_sq0"), rows("uc_sq0"), rows("ucd_sq0")
-        nc.gpsimd.tensor_tensor(out=ab_sq0[:], in0=ab0[:], in1=ab0[:], op=ALU.mult)
-        nc.scalar.activation(out=uc_sq0[:], in_=uc0[:], func=ACT.Square, scale=math.sqrt(1.0 / 3.0))
-        nc.scalar.activation(out=ucd_sq0[:], in_=ucd0[:], func=ACT.Square, scale=math.sqrt(8.0 / 3.0))
-        var0 = bank("var0", "u0")
-        sum0 = bank("sum0", "a0")
+        nc.gpsimd.tensor_tensor(out=uc_sq0[:], in0=uc0[:], in1=uc0[:], op=ALU.mult)
+        nc.scalar.activation(out=ucd_sq0[:], in_=ucd0[:], func=ACT.Square, scale=math.sqrt(2.0))
+        var0 = bank("var0", "a0")
+        sum0 = bank("sum0", "u0")
         turn(sum0, three0, opens=True)
         turn(var0, ab_sq0, opens=True)
         turn(sum0, ucd0, closes=True)
-        turn(var0, uc_sq0)
-        turn(var0, ucd_sq0, closes=True)
+        turn(var0, ucd_sq0)
+        turn(var0, uc_sq0, closes=True)
 
-        ab1, uc1, three1, ucd1 = work("ab1"), work("uc1"), work("three1"), work("ucd1")
+        ab1, uc1, three1, ucd1 = work("ab1"), work("uc1"), work("three1", "three1"), work("ucd1")
         ab_sq1, uc_sq1 = work("ab_sq1"), work("uc_sq1", "uc_sq1")
         combine(ab1[:], bank_a[1], 0.5, u1, ALU.subtract)
         nc.scalar.activation(out=ab_sq1[:], in_=ab1[:], func=ACT.Square, scale=math.sqrt(6.0))
@@ -231,7 +245,7 @@ def tile_picked_statpool_none_e_kernel(tc, xT, w1, w2_words, w2_scales, w3_words
                 nc.vector.scalar_tensor_tensor(
                     out=dst[:, cols], in0=woven(src)[:, cols], scalar=factor, in1=other[:, cols], op0=ALU.mult, op1=ALU.add
                 )
-        mean_b = keep.tile([P, 2, VH, PACK], BF16, name="mean_b", align_bytes=64)
+        mean_b = keep.tile([P, 2, VH, PACK], BF16, name="mean_b", tag="late", align_bytes=64)
         nc.scalar.activation(out=mean_b[:, 0], in_=woven(sum0), func=ACT.Copy, scale=0.25)
         ucd_sq1 = [work("ucd_sq_1_%d" % c, "ucd_sq_1_%d" % c, VH // 2) for c in range(2)]
         for c, cols in enumerate(parts(2)):
@@ -242,10 +256,10 @@ def tile_picked_statpool_none_e_kernel(tc, xT, w1, w2_words, w2_scales, w3_words
         for engine, cols in zip((nc.gpsimd, nc.vector), (slice(0, 3 * VH // 4), slice(3 * VH // 4, VH))):
             engine.tensor_tensor(out=two1[:, cols], in0=ab_sq1[:, cols], in1=uc_sq1[:, cols], op=ALU.add)
         dev_b = [
-            keep.tile([P, VH, PACK], BF16, name="dev_b0", align_bytes=64),
+            keep.tile([P, VH, PACK], BF16, name="dev_b0", tag="three1", align_bytes=64),
             keep.tile([P, VH, PACK], BF16, name="dev_b1", align_bytes=64),
         ]
-        nc.scalar.activation(out=dev_b[0][:], in_=woven(var0), func=ACT.Sqrt, scale=9.0 / 128.0)
+        nc.scalar.activation(out=dev_b[0][:], in_=woven(var0), func=ACT.Sqrt, scale=3.0 / 32.0)
         total1 = work("total1")
         for c, cols in enumerate(parts(4)):
             nc.vector.tensor_tensor(out=total1[:, cols], in0=two1[:, cols], in1=ucd_sq1[c // 2][:, parts(4)[c % 2]], op=ALU.add)

@@ -23,6 +23,7 @@ D = 4
 VH = 128
 W_CHUNKS = 4
 QUADRANTS = 4
+GPSIMD_SHARE = 3 * VH // 4
 
 
 def parts(n):
@@ -44,7 +45,7 @@ def tile_picked_statpool_none_e_kernel(tc, xT, w1, w2_words, w2_scales, w3_words
             nc.sync.dma_start(out=planes[j][:], in_=x_rows[:, j, :])
         w_rows = w1.rearrange("(p j) c -> p j c", j=PACK)
         chunk = H // W_CHUNKS
-        w_raw = [keep.tile([P, PACK, chunk], F32, name="w_raw%d" % c, tag="w_raw%d" % c, align_bytes=64) for c in range(W_CHUNKS)]
+        w_raw = [keep.tile([P, PACK, chunk], F32, name="w_raw%d" % c, align_bytes=64) for c in range(W_CHUNKS)]
         for c in range(W_CHUNKS):
             nc.sync.dma_start(out=w_raw[c][:], in_=w_rows[:, :, c * chunk : (c + 1) * chunk])
 
@@ -65,25 +66,24 @@ def tile_picked_statpool_none_e_kernel(tc, xT, w1, w2_words, w2_scales, w3_words
                     out=scale_tile[32 * r : 32 * r + 4, :].bitcast(I32), in_=scale_rows[0, 4 * r : 4 * r + 4, :].bitcast(I32)
                 )
             tail_scales.append(scale_tile)
+
         identity = keep.tile([P, P], F32, name="identity")
         make_identity(nc, identity[:])
 
-        stage = keep.tile([P, 8, D * VH * PACK], BF16, name="stage", align_bytes=64)
-        picked = stage[:, 0:4:2, :].rearrange("p h (d v j) -> p h d v j", d=D, j=PACK)
-        w_grouped = stage[:, 1:8:2, : P * PACK].rearrange("p t (m j) -> p t m j", j=PACK)
+        stage = keep.tile([P, 2 * PACK, D * VH * PACK], BF16, name="stage", align_bytes=64)
+        picked = stage[:, 0:3:2, :].rearrange("p h (d v j) -> p h d v j", d=D, j=PACK)
+        w_grouped = stage[:, 1::2, : P * PACK].rearrange("p t (m j) -> p t m j", j=PACK)
 
         last_plane = PACK - 1
-        pair_columns = 3 * S // 16 // D
+        abc_columns = (D - 1) * S // 16 // D
         for j in range(last_plane):
             nc.vector.tensor_copy(out=picked[:, :, :, :, j].rearrange("p h d v -> p d h v"), in_=planes[j][:].indirect(offsets[:]))
         nc.vector.tensor_copy(
-            out=picked[:, :, 0:3, :, last_plane].rearrange("p h d v -> p d h v"),
-            in_=planes[last_plane][:].indirect(offsets[:, :pair_columns]),
+            out=picked[:, :, : D - 1, :, last_plane].rearrange("p h d v -> p d h v"),
+            in_=planes[last_plane][:].indirect(offsets[:, :abc_columns]),
         )
-        late_cd = keep.tile([P, 2, VH], BF16, name="late_cd", align_bytes=64)
-        nc.vector.tensor_copy(
-            out=late_cd[:].rearrange("p h v -> p (h v)"), in_=planes[last_plane][:].indirect(offsets[:, pair_columns:])
-        )
+        late_d = keep.tile([P, 2, VH], BF16, name="late_d", align_bytes=64)
+        nc.vector.tensor_copy(out=late_d[:].rearrange("p h v -> p (h v)"), in_=planes[last_plane][:].indirect(offsets[:, abc_columns:]))
 
         def round_w(c, slices):
             nc.scalar.copy(
@@ -107,6 +107,7 @@ def tile_picked_statpool_none_e_kernel(tc, xT, w1, w2_words, w2_scales, w3_words
             return codes, scales
 
         x_ab0 = quantize(picked[:, 0, 0:2].rearrange("p d v j -> p (d v j)"), 2 * VH, "x_ab0")
+        x_c0 = quantize(picked[:, 0, 2].rearrange("p v j -> p (v j)"), VH, "x_c0")
         w_q = mx_tiles(H, "w")
         for t in range(PACK):
             nc.vector.quantize_mx(
@@ -114,156 +115,141 @@ def tile_picked_statpool_none_e_kernel(tc, xT, w1, w2_words, w2_scales, w3_words
                 scales=w_q[1][:, t * P : (t + 1) * P],
                 in_=w_grouped[:, t].rearrange("p m j -> p (m j)"),
             )
-        nc.scalar.copy(out=picked[:, :, 3, :, last_plane], in_=late_cd[:])
-        x_c0 = quantize(picked[:, 0, 2].rearrange("p v j -> p (v j)"), VH, "x_c0", tag="w_raw2")
-        x_abc1 = mx_tiles(3 * VH, "x_abc1", tag="w_raw%d" % (W_CHUNKS - 1))
-        for pieces in (slice(0, 2), slice(2, 3)):
-            cols = slice(pieces.start * VH, pieces.stop * VH)
-            nc.vector.quantize_mx(
-                out=x_abc1[0][:, cols].bitcast(FP8X4),
-                scales=x_abc1[1][:, cols],
-                in_=picked[:, 1, pieces].rearrange("p d v j -> p (d v j)"),
-            )
+        nc.scalar.copy(out=picked[:, :, D - 1, :, last_plane], in_=late_d[:])
+        x_ab1 = quantize(picked[:, 1, 0:2].rearrange("p d v j -> p (d v j)"), 2 * VH, "x_ab1")
+        x_c1 = quantize(picked[:, 1, 2].rearrange("p v j -> p (v j)"), VH, "x_c1")
         x_d0 = quantize(picked[:, 0, 3].rearrange("p v j -> p (v j)"), VH, "x_d0")
         x_d1 = quantize(picked[:, 1, 3].rearrange("p v j -> p (v j)"), VH, "x_d1")
 
         x_q = (
             ((x_ab0, 0), (x_ab0, 1), (x_c0, 0), (x_d0, 0)),
-            ((x_abc1, 0), (x_abc1, 1), (x_abc1, 2), (x_d1, 0)),
+            ((x_ab1, 0), (x_ab1, 1), (x_c1, 0), (x_d1, 0)),
         )
 
-        def product(dst, pieces, half):
+        def product_by_segments(dst, piece, slices=slice(0, PACK)):
+            (codes, scales), place = x_q[0][piece]
+            frames = slice(place * VH, (place + 1) * VH)
+            cols = slice(slices.start * P, slices.stop * P)
+            nc.tensor.matmul_mx(
+                out=dst[:].rearrange("p t m -> p (t m)")[:, cols],
+                lhsT=codes[:, frames].bitcast(FP8X4),
+                lhsT_scale=scales[:, frames],
+                rhs=w_q[0][:, cols].bitcast(FP8X4),
+                rhs_scale=w_q[1][:, cols],
+                start=True,
+                stop=True,
+            )
+
+        def product_by_channels(dst, pieces):
             for t in range(PACK):
                 for n, piece in enumerate(pieces):
-                    (codes, scales), place = x_q[half][piece]
-                    cols = slice(place * VH, (place + 1) * VH)
+                    (codes, scales), place = x_q[1][piece]
+                    frames = slice(place * VH, (place + 1) * VH)
                     nc.tensor.matmul_mx(
                         out=dst[:, t, :],
                         lhsT=w_q[0][:, t * P : (t + 1) * P].bitcast(FP8X4),
                         lhsT_scale=w_q[1][:, t * P : (t + 1) * P],
-                        rhs=codes[:, cols].bitcast(FP8X4),
-                        rhs_scale=scales[:, cols],
+                        rhs=codes[:, frames].bitcast(FP8X4),
+                        rhs_scale=scales[:, frames],
                         start=(n == 0),
                         stop=(n == len(pieces) - 1),
                     )
 
-        def product_turned(dst, pieces, slices=slice(0, PACK), place_in=None):
-            cols = slice(slices.start * P, slices.stop * P)
-            place_in = place_in or slices
-            dst_cols = slice(place_in.start * P, place_in.stop * P)
-            for n, piece in enumerate(pieces):
-                (codes, scales), place = x_q[0][piece]
-                frames = slice(place * VH, (place + 1) * VH)
-                nc.tensor.matmul_mx(
-                    out=dst[:].rearrange("p t m -> p (t m)")[:, dst_cols],
-                    lhsT=codes[:, frames].bitcast(FP8X4),
-                    lhsT_scale=scales[:, frames],
-                    rhs=w_q[0][:, cols].bitcast(FP8X4),
-                    rhs_scale=w_q[1][:, cols],
-                    start=(n == 0),
-                    stop=(n == len(pieces) - 1),
+        def turn(dst, src, opens=False, closes=False):
+            for t in range(PACK):
+                nc.tensor.matmul(
+                    dst[:, t, :],
+                    lhsT=src[:, t, :],
+                    rhs=identity[:],
+                    is_transpose=True,
+                    start=(opens and t == 0),
+                    stop=(closes and t == PACK - 1),
                 )
 
         def woven(src):
             return src[:].rearrange("p t v -> p v t")
 
-        def work(name, tag="", width=VH):
-            return keep.tile([P, width, PACK], F32, name=name, tag=tag, align_bytes=64)
-
-        def bank(name, tag=""):
+        def bank(name, tag):
             return psum.tile([P, PACK, VH], F32, name=name, tag=tag)
 
-        def combine(dst, src, factor, other, op1=ALU.add):
-            nc.vector.scalar_tensor_tensor(out=dst, in0=woven(src), scalar=factor, in1=other[:], op0=ALU.mult, op1=op1)
+        def by_segments(name, tag=""):
+            return keep.tile([P, PACK, P], F32, name=name, tag=tag, align_bytes=64)
 
-        bank_u = [bank("bank_b0", "u0"), bank("bank_u1", "u1")]
+        def by_channels(name, tag="", width=VH):
+            return keep.tile([P, width, PACK], F32, name=name, tag=tag, align_bytes=64)
+
+        def combine(dst, src, factor, other, op1=ALU.add):
+            nc.vector.scalar_tensor_tensor(out=dst, in0=src, scalar=factor, in1=other, op0=ALU.mult, op1=op1)
+
+        bank_b0, bank_u1 = bank("bank_b0", "b0"), bank("bank_u1", "u1")
         bank_a = [bank("bank_a%d" % half, "a%d" % half) for half in range(2)]
         bank_c = [bank("bank_c%d" % half, "c%d" % half) for half in range(2)]
         bank_d = [bank("bank_d%d" % half, "d%d" % half) for half in range(2)]
-
-        def rows(name, tag=""):
-            return keep.tile([P, PACK, P], F32, name=name, tag=tag, align_bytes=64)
-
-        a0 = rows("a0", "sums")
-        u1 = work("u1", "late")
+        a0 = by_segments("a0")
+        u1 = by_channels("u1", "u1")
         for t in range(PACK):
-            product_turned(bank_a[0], (0,), slice(t, t + 1))
+            product_by_segments(bank_a[0], 0, slice(t, t + 1))
         nc.scalar.activation(out=a0[:], in_=bank_a[0][:], func=ACT.Copy, scale=4.0 / 3.0)
-        product_turned(bank_u[0], (1,))
-        product_turned(bank_c[0], (2,))
-        product(bank_u[1], (0, 1), 1)
-        nc.scalar.activation(out=u1[:], in_=woven(bank_u[1]), func=ACT.Copy, scale=0.25)
-        product_turned(bank_d[0], (3,))
-        product(bank_a[1], (0,), 1)
-        product(bank_c[1], (2,), 1)
-        product(bank_d[1], (3,), 1)
+        product_by_segments(bank_b0, 1)
+        product_by_segments(bank_c[0], 2)
+        product_by_channels(bank_u1, (0, 1))
+        nc.scalar.activation(out=u1[:], in_=woven(bank_u1), func=ACT.Copy, scale=0.25)
+        product_by_segments(bank_d[0], 3)
+        product_by_channels(bank_a[1], (0,))
+        product_by_channels(bank_c[1], (2,))
+        product_by_channels(bank_d[1], (3,))
 
-        def from_bank(name, src, factor, other, op1):
-            dst = rows(name, name)
-            nc.vector.scalar_tensor_tensor(out=dst[:], in0=src[:], scalar=factor, in1=other[:], op0=ALU.mult, op1=op1)
-            return dst
-
-        def turn(dst, src, opens=False, closes=False):
-            for t in range(PACK):
-                nc.tensor.matmul(
-                    dst[:, t, :], lhsT=src[:, t, :], rhs=identity[:], is_transpose=True,
-                    start=(opens and t == 0), stop=(closes and t == PACK - 1),
-                )
-
-        u0, three0 = rows("u0"), rows("three0")
-        for dst, src, other in ((u0, bank_u[0], a0), (three0, bank_c[0], u0)):
-            for pair in (slice(0, 2), slice(2, 4)):
-                nc.vector.scalar_tensor_tensor(
-                    out=dst[:, pair], in0=src[:, pair], scalar=4.0 / 3.0, in1=other[:, pair], op0=ALU.mult, op1=ALU.add
-                )
-        ab0 = from_bank("ab0", bank_u[0], 4.0 / 3.0, a0, ALU.subtract)
-        ab_sq0, uc_sq0, ucd_sq0 = rows("ab_sq0"), rows("uc_sq0"), rows("ucd_sq0")
+        u0, three0 = by_segments("u0"), by_segments("three0")
+        for dst, src, other in ((u0, bank_b0, a0), (three0, bank_c[0], u0)):
+            for pair in (slice(0, 2), slice(2, PACK)):
+                combine(dst[:, pair], src[:, pair], 4.0 / 3.0, other[:, pair])
+        ab0 = by_segments("ab0")
+        combine(ab0[:], bank_b0[:], 4.0 / 3.0, a0[:], ALU.subtract)
+        ab_sq0, uc_sq0, ucd_sq0 = by_segments("ab_sq0"), by_segments("uc_sq0"), by_segments("ucd_sq0")
         nc.scalar.activation(out=ab_sq0[:], in_=ab0[:], func=ACT.Square, scale=math.sqrt(0.75))
-        u0_twice, uc0 = rows("u0_twice"), rows("uc0")
+        u0_twice, uc0 = by_segments("u0_twice"), by_segments("uc0")
         nc.gpsimd.tensor_scalar(out=u0_twice[:], in0=u0[:], scalar1=1.5, scalar2=0.0, op0=ALU.mult, op1=ALU.add)
         nc.gpsimd.tensor_tensor(out=uc0[:], in0=three0[:], in1=u0_twice[:], op=ALU.subtract)
-        ucd0 = rows("ucd0")
-        nc.vector.scalar_tensor_tensor(out=ucd0[:], in0=three0[:], scalar=-0.25, in1=bank_d[0][:], op0=ALU.mult, op1=ALU.add)
+        ucd0 = by_segments("ucd0")
+        combine(ucd0[:], three0[:], -0.25, bank_d[0][:])
         nc.gpsimd.tensor_tensor(out=uc_sq0[:], in0=uc0[:], in1=uc0[:], op=ALU.mult)
         nc.scalar.activation(out=ucd_sq0[:], in_=ucd0[:], func=ACT.Square, scale=math.sqrt(2.0))
-        var0 = bank("var0", "a0")
-        sum0 = bank("sum0", "u0")
+        squares0 = bank("squares0", "a0")
+        sum0 = bank("sum0", "b0")
         turn(sum0, three0, opens=True)
-        turn(var0, ab_sq0, opens=True)
+        turn(squares0, ab_sq0, opens=True)
         turn(sum0, ucd0, closes=True)
-        turn(var0, ucd_sq0)
-        turn(var0, uc_sq0, closes=True)
+        turn(squares0, ucd_sq0)
+        turn(squares0, uc_sq0, closes=True)
 
-        ab1, uc1, three1, ucd1 = work("ab1"), work("uc1"), work("three1", "three1"), work("ucd1")
-        ab_sq1, uc_sq1 = work("ab_sq1"), work("uc_sq1", "uc_sq1")
-        combine(ab1[:], bank_a[1], 0.5, u1, ALU.subtract)
+        ab1, uc1, three1, ucd1 = by_channels("ab1"), by_channels("uc1"), by_channels("three1", "three1"), by_channels("ucd1")
+        ab_sq1, uc_sq1 = by_channels("ab_sq1"), by_channels("uc_sq1")
+        combine(ab1[:], woven(bank_a[1]), 0.5, u1[:], ALU.subtract)
         nc.scalar.activation(out=ab_sq1[:], in_=ab1[:], func=ACT.Square, scale=math.sqrt(6.0))
-        combine(uc1[:], bank_c[1], -0.5, u1)
+        combine(uc1[:], woven(bank_c[1]), -0.5, u1[:])
         nc.scalar.activation(out=uc_sq1[:], in_=uc1[:], func=ACT.Square, scale=math.sqrt(2.0))
         for dst, src, factor, other in ((three1, bank_c[1], 0.25, u1), (ucd1, bank_d[1], -0.75, three1)):
             for cols in parts(2):
-                nc.vector.scalar_tensor_tensor(
-                    out=dst[:, cols], in0=woven(src)[:, cols], scalar=factor, in1=other[:, cols], op0=ALU.mult, op1=ALU.add
-                )
-        mean_b = keep.tile([P, 2, VH, PACK], BF16, name="mean_b", tag="late", align_bytes=64)
+                combine(dst[:, cols], woven(src)[:, cols], factor, other[:, cols])
+
+        mean_b = keep.tile([P, 2, VH, PACK], BF16, name="mean_b", tag="u1", align_bytes=64)
         nc.scalar.activation(out=mean_b[:, 0], in_=woven(sum0), func=ACT.Copy, scale=0.25)
-        ucd_sq1 = [work("ucd_sq_1_%d" % c, "ucd_sq_1_%d" % c, VH // 2) for c in range(2)]
+        ucd_sq1 = [by_channels("ucd_sq1_%d" % c, "ucd_sq1_%d" % c, VH // 2) for c in range(2)]
         for c, cols in enumerate(parts(2)):
             nc.scalar.activation(out=ucd_sq1[c][:], in_=ucd1[:, cols], func=ACT.Square)
-
-        combine(mean_b[:, 1], bank_d[1], 0.25, three1)
-        two1 = work("two_1", "two_1")
-        for engine, cols in zip((nc.gpsimd, nc.vector), (slice(0, 3 * VH // 4), slice(3 * VH // 4, VH))):
+        combine(mean_b[:, 1], woven(bank_d[1]), 0.25, three1[:])
+        two1 = by_channels("two1", "two1")
+        for engine, cols in ((nc.gpsimd, slice(0, GPSIMD_SHARE)), (nc.vector, slice(GPSIMD_SHARE, VH))):
             engine.tensor_tensor(out=two1[:, cols], in0=ab_sq1[:, cols], in1=uc_sq1[:, cols], op=ALU.add)
         dev_b = [
             keep.tile([P, VH, PACK], BF16, name="dev_b0", tag="three1", align_bytes=64),
             keep.tile([P, VH, PACK], BF16, name="dev_b1", align_bytes=64),
         ]
-        nc.scalar.activation(out=dev_b[0][:], in_=woven(var0), func=ACT.Sqrt, scale=3.0 / 32.0)
-        total1 = work("total1")
+        nc.scalar.activation(out=dev_b[0][:], in_=woven(squares0), func=ACT.Sqrt, scale=3.0 / 32.0)
+        squares1 = by_channels("squares1")
         for c, cols in enumerate(parts(4)):
-            nc.vector.tensor_tensor(out=total1[:, cols], in0=two1[:, cols], in1=ucd_sq1[c // 2][:, parts(4)[c % 2]], op=ALU.add)
-            nc.scalar.activation(out=dev_b[1][:, cols], in_=total1[:, cols], func=ACT.Sqrt, scale=1.0 / 3.0)
+            nc.vector.tensor_tensor(out=squares1[:, cols], in0=two1[:, cols], in1=ucd_sq1[c // 2][:, parts(4)[c % 2]], op=ALU.add)
+            nc.scalar.activation(out=dev_b[1][:, cols], in_=squares1[:, cols], func=ACT.Sqrt, scale=1.0 / 3.0)
 
         def finish(half, mean_q, dev_q):
             cols = slice(half * VH, (half + 1) * VH)
@@ -282,8 +268,8 @@ def tile_picked_statpool_none_e_kernel(tc, xT, w1, w2_words, w2_scales, w3_words
             nc.scalar.copy(out=result[:], in_=acc[:])
             nc.sync.dma_start(out=out[:, cols], in_=result[:])
 
-        means_q = quantize(mean_b[:].rearrange("p h v t -> p (h v t)"), 2 * VH, "mean", tag="ucd_sq_1_0")
-        dev0_q = quantize(dev_b[0][:].rearrange("p v t -> p (v t)"), VH, "dev0", tag="two_1")
+        means_q = quantize(mean_b[:].rearrange("p h v t -> p (h v t)"), 2 * VH, "mean", tag="ucd_sq1_0")
+        dev0_q = quantize(dev_b[0][:].rearrange("p v t -> p (v t)"), VH, "dev0", tag="two1")
         finish(0, means_q, dev0_q)
         dev1_q = mx_tiles(VH, "dev1")
         for cols in parts(2):

import math
from contextlib import ExitStack

import concourse.mybir as mybir
from concourse.masks import make_identity

K, T, S, V, H, N = 512, 4096, 1024, 256, 512, 128
FLOPS = 2 * K * H * S + 2 * 2 * H * N * V

F32 = mybir.dt.float32
BF16 = mybir.dt.bfloat16
I32 = mybir.dt.int32
U32 = mybir.dt.uint32
U16 = mybir.dt.uint16
U8 = mybir.dt.uint8
FP8X4 = mybir.dt.float8_e4m3fn_x4
ACT = mybir.ActivationFunctionType
ALU = mybir.AluOpType

P = 128
PACK = 4
D = 4
VH = 128
W_CHUNKS = 4
QUADRANTS = 4
GPSIMD_SHARE = 3 * VH // 4


def parts(n):
    return [slice(c * VH // n, (c + 1) * VH // n) for c in range(n)]


def tile_picked_statpool_none_e_kernel(tc, xT, w1, w2_words, w2_scales, w3_words, w3_scales, offs, out):
    nc = tc.nc
    with ExitStack() as ctx:
        keep = ctx.enter_context(tc.tile_pool(name="keep", bufs=1))
        psum = ctx.enter_context(tc.psum_pool(name="psum", bufs=1))

        x_rows = xT.rearrange("(p j) t -> p j t", j=PACK)
        planes = [keep.tile([P, T], F32, name="plane%d" % j) for j in range(PACK)]
        offsets = keep.tile([P, S // 16], U16, name="offsets")
        nc.sync.dma_start(out=planes[0][:], in_=x_rows[:, 0, :])
        nc.sync.dma_start(offsets[:], offs)
        for j in range(1, PACK):
            nc.sync.dma_start(out=planes[j][:], in_=x_rows[:, j, :])
        w_rows = w1.rearrange("(p j) c -> p j c", j=PACK)
        chunk = H // W_CHUNKS
        w_raw = [keep.tile([P, PACK, chunk], F32, name="w_raw%d" % c, align_bytes=64) for c in range(W_CHUNKS)]
        for c in range(W_CHUNKS):
            nc.sync.dma_start(out=w_raw[c][:], in_=w_rows[:, :, c * chunk : (c + 1) * chunk])

        tail_words = []
        tail_scales = []
        for i, words in enumerate((w2_words, w3_words)):
            word_tile = keep.tile([P, N], I32, name="tail_words%d" % i, align_bytes=64)
            nc.sync.dma_start(out=word_tile[:], in_=words[0].rearrange("p n t -> p (n t)").bitcast(I32))
            tail_words.append(word_tile)
        for i, scale_rows in enumerate((w2_scales, w3_scales)):
            scale_tile = keep.tile([P, N], U8, name="tail_scales%d" % i, align_bytes=64)
            nc.gpsimd.memset(scale_tile[:], 0)
            if i == 0:
                warm = keep.tile([P, 1], F32, name="warm")
                nc.scalar.activation(out=warm[:], in_=scale_tile[:, 0:4].bitcast(F32), func=ACT.Sqrt)
            for r in range(QUADRANTS):
                nc.sync.dma_start(
                    out=scale_tile[32 * r : 32 * r + 4, :].bitcast(I32), in_=scale_rows[0, 4 * r : 4 * r + 4, :].bitcast(I32)
                )
            tail_scales.append(scale_tile)

        identity = keep.tile([P, P], F32, name="identity")
        make_identity(nc, identity[:])

        stage = keep.tile([P, 2 * PACK, D * VH * PACK], BF16, name="stage", align_bytes=64)
        picked = stage[:, 0:3:2, :].rearrange("p h (d v j) -> p h d v j", d=D, j=PACK)
        w_grouped = stage[:, 1::2, : P * PACK].rearrange("p t (m j) -> p t m j", j=PACK)

        last_plane = PACK - 1
        abc_columns = (D - 1) * S // 16 // D
        for j in range(last_plane):
            nc.vector.tensor_copy(out=picked[:, :, :, :, j].rearrange("p h d v -> p d h v"), in_=planes[j][:].indirect(offsets[:]))
        nc.vector.tensor_copy(
            out=picked[:, :, : D - 1, :, last_plane].rearrange("p h d v -> p d h v"),
            in_=planes[last_plane][:].indirect(offsets[:, :abc_columns]),
        )
        late_d = keep.tile([P, 2, VH], BF16, name="late_d", align_bytes=64)
        nc.vector.tensor_copy(out=late_d[:].rearrange("p h v -> p (h v)"), in_=planes[last_plane][:].indirect(offsets[:, abc_columns:]))

        def round_w(c, slices):
            nc.scalar.copy(
                out=w_grouped[:, slices, c * chunk // PACK : (c + 1) * chunk // PACK, :].rearrange("p t m j -> p m j t"),
                in_=w_raw[c][:].rearrange("p j (m t) -> p m j t", t=PACK)[:, :, :, slices],
            )

        for c in range(W_CHUNKS - 1):
            round_w(c, slice(0, PACK))
        round_w(W_CHUNKS - 1, slice(0, 2))
        round_w(W_CHUNKS - 1, slice(2, PACK))

        def mx_tiles(width, name, tag=""):
            codes = keep.tile([P, width], U32, name=name + "_codes", tag=tag, align_bytes=64)
            scales = keep.tile([P, width], U8, name=name + "_scales", align_bytes=64)
            return codes, scales

        def quantize(src, width, name, tag=""):
            codes, scales = mx_tiles(width, name, tag)
            nc.vector.quantize_mx(out=codes[:].bitcast(FP8X4), scales=scales[:], in_=src)
            return codes, scales

        x_ab0 = quantize(picked[:, 0, 0:2].rearrange("p d v j -> p (d v j)"), 2 * VH, "x_ab0")
        x_c0 = quantize(picked[:, 0, 2].rearrange("p v j -> p (v j)"), VH, "x_c0")
        w_q = mx_tiles(H, "w")
        for t in range(PACK):
            nc.vector.quantize_mx(
                out=w_q[0][:, t * P : (t + 1) * P].bitcast(FP8X4),
                scales=w_q[1][:, t * P : (t + 1) * P],
                in_=w_grouped[:, t].rearrange("p m j -> p (m j)"),
            )
        nc.scalar.copy(out=picked[:, :, D - 1, :, last_plane], in_=late_d[:])
        x_ab1 = quantize(picked[:, 1, 0:2].rearrange("p d v j -> p (d v j)"), 2 * VH, "x_ab1")
        x_c1 = quantize(picked[:, 1, 2].rearrange("p v j -> p (v j)"), VH, "x_c1")
        x_d0 = quantize(picked[:, 0, 3].rearrange("p v j -> p (v j)"), VH, "x_d0")
        x_d1 = quantize(picked[:, 1, 3].rearrange("p v j -> p (v j)"), VH, "x_d1")

        x_q = (
            ((x_ab0, 0), (x_ab0, 1), (x_c0, 0), (x_d0, 0)),
            ((x_ab1, 0), (x_ab1, 1), (x_c1, 0), (x_d1, 0)),
        )

        def product_by_segments(dst, piece, slices=slice(0, PACK)):
            (codes, scales), place = x_q[0][piece]
            frames = slice(place * VH, (place + 1) * VH)
            cols = slice(slices.start * P, slices.stop * P)
            nc.tensor.matmul_mx(
                out=dst[:].rearrange("p t m -> p (t m)")[:, cols],
                lhsT=codes[:, frames].bitcast(FP8X4),
                lhsT_scale=scales[:, frames],
                rhs=w_q[0][:, cols].bitcast(FP8X4),
                rhs_scale=w_q[1][:, cols],
                start=True,
                stop=True,
            )

        def product_by_channels(dst, pieces):
            for t in range(PACK):
                for n, piece in enumerate(pieces):
                    (codes, scales), place = x_q[1][piece]
                    frames = slice(place * VH, (place + 1) * VH)
                    nc.tensor.matmul_mx(
                        out=dst[:, t, :],
                        lhsT=w_q[0][:, t * P : (t + 1) * P].bitcast(FP8X4),
                        lhsT_scale=w_q[1][:, t * P : (t + 1) * P],
                        rhs=codes[:, frames].bitcast(FP8X4),
                        rhs_scale=scales[:, frames],
                        start=(n == 0),
                        stop=(n == len(pieces) - 1),
                    )

        def turn(dst, src, opens=False, closes=False):
            for t in range(PACK):
                nc.tensor.matmul(
                    dst[:, t, :],
                    lhsT=src[:, t, :],
                    rhs=identity[:],
                    is_transpose=True,
                    start=(opens and t == 0),
                    stop=(closes and t == PACK - 1),
                )

        def woven(src):
            return src[:].rearrange("p t v -> p v t")

        def bank(name, tag):
            return psum.tile([P, PACK, VH], F32, name=name, tag=tag)

        def by_segments(name, tag=""):
            return keep.tile([P, PACK, P], F32, name=name, tag=tag, align_bytes=64)

        def by_channels(name, tag="", width=VH):
            return keep.tile([P, width, PACK], F32, name=name, tag=tag, align_bytes=64)

        def combine(dst, src, factor, other, op1=ALU.add):
            nc.vector.scalar_tensor_tensor(out=dst, in0=src, scalar=factor, in1=other, op0=ALU.mult, op1=op1)

        bank_b0, bank_u1 = bank("bank_b0", "b0"), bank("bank_u1", "u1")
        bank_a = [bank("bank_a%d" % half, "a%d" % half) for half in range(2)]
        bank_c = [bank("bank_c%d" % half, "c%d" % half) for half in range(2)]
        bank_d = [bank("bank_d%d" % half, "d%d" % half) for half in range(2)]
        a0 = by_segments("a0")
        u1 = by_channels("u1", "u1")
        for t in range(PACK):
            product_by_segments(bank_a[0], 0, slice(t, t + 1))
        nc.scalar.activation(out=a0[:], in_=bank_a[0][:], func=ACT.Copy, scale=4.0 / 3.0)
        product_by_segments(bank_b0, 1)
        product_by_segments(bank_c[0], 2)
        product_by_channels(bank_u1, (0, 1))
        nc.scalar.activation(out=u1[:], in_=woven(bank_u1), func=ACT.Copy, scale=0.25)
        product_by_segments(bank_d[0], 3)
        product_by_channels(bank_a[1], (0,))
        product_by_channels(bank_c[1], (2,))
        product_by_channels(bank_d[1], (3,))

        u0, three0 = by_segments("u0"), by_segments("three0")
        for dst, src, other in ((u0, bank_b0, a0), (three0, bank_c[0], u0)):
            for pair in (slice(0, 2), slice(2, PACK)):
                combine(dst[:, pair], src[:, pair], 4.0 / 3.0, other[:, pair])
        ab0 = by_segments("ab0")
        combine(ab0[:], bank_b0[:], 4.0 / 3.0, a0[:], ALU.subtract)
        ab_sq0, uc_sq0, ucd_sq0 = by_segments("ab_sq0"), by_segments("uc_sq0"), by_segments("ucd_sq0")
        nc.scalar.activation(out=ab_sq0[:], in_=ab0[:], func=ACT.Square, scale=math.sqrt(0.75))
        u0_twice, uc0 = by_segments("u0_twice"), by_segments("uc0")
        nc.gpsimd.tensor_scalar(out=u0_twice[:], in0=u0[:], scalar1=1.5, scalar2=0.0, op0=ALU.mult, op1=ALU.add)
        nc.gpsimd.tensor_tensor(out=uc0[:], in0=three0[:], in1=u0_twice[:], op=ALU.subtract)
        ucd0 = by_segments("ucd0")
        combine(ucd0[:], three0[:], -0.25, bank_d[0][:])
        nc.gpsimd.tensor_tensor(out=uc_sq0[:], in0=uc0[:], in1=uc0[:], op=ALU.mult)
        nc.scalar.activation(out=ucd_sq0[:], in_=ucd0[:], func=ACT.Square, scale=math.sqrt(2.0))
        squares0 = bank("squares0", "a0")
        sum0 = bank("sum0", "b0")
        turn(sum0, three0, opens=True)
        turn(squares0, ab_sq0, opens=True)
        turn(sum0, ucd0, closes=True)
        turn(squares0, ucd_sq0)
        turn(squares0, uc_sq0, closes=True)

        ab1, uc1, three1, ucd1 = by_channels("ab1"), by_channels("uc1"), by_channels("three1", "three1"), by_channels("ucd1")
        ab_sq1, uc_sq1 = by_channels("ab_sq1"), by_channels("uc_sq1")
        combine(ab1[:], woven(bank_a[1]), 0.5, u1[:], ALU.subtract)
        nc.scalar.activation(out=ab_sq1[:], in_=ab1[:], func=ACT.Square, scale=math.sqrt(6.0))
        combine(uc1[:], woven(bank_c[1]), -0.5, u1[:])
        nc.scalar.activation(out=uc_sq1[:], in_=uc1[:], func=ACT.Square, scale=math.sqrt(2.0))
        for dst, src, factor, other in ((three1, bank_c[1], 0.25, u1), (ucd1, bank_d[1], -0.75, three1)):
            for cols in parts(2):
                combine(dst[:, cols], woven(src)[:, cols], factor, other[:, cols])

        mean_b = keep.tile([P, 2, VH, PACK], BF16, name="mean_b", tag="u1", align_bytes=64)
        nc.scalar.activation(out=mean_b[:, 0], in_=woven(sum0), func=ACT.Copy, scale=0.25)
        ucd_sq1 = [by_channels("ucd_sq1_%d" % c, "ucd_sq1_%d" % c, VH // 2) for c in range(2)]
        for c, cols in enumerate(parts(2)):
            nc.scalar.activation(out=ucd_sq1[c][:], in_=ucd1[:, cols], func=ACT.Square)
        combine(mean_b[:, 1], woven(bank_d[1]), 0.25, three1[:])
        two1 = by_channels("two1", "two1")
        for engine, cols in ((nc.gpsimd, slice(0, GPSIMD_SHARE)), (nc.vector, slice(GPSIMD_SHARE, VH))):
            engine.tensor_tensor(out=two1[:, cols], in0=ab_sq1[:, cols], in1=uc_sq1[:, cols], op=ALU.add)
        dev_b = [
            keep.tile([P, VH, PACK], BF16, name="dev_b0", tag="three1", align_bytes=64),
            keep.tile([P, VH, PACK], BF16, name="dev_b1", align_bytes=64),
        ]
        nc.scalar.activation(out=dev_b[0][:], in_=woven(squares0), func=ACT.Sqrt, scale=3.0 / 32.0)
        squares1 = by_channels("squares1")
        for c, cols in enumerate(parts(4)):
            nc.vector.tensor_tensor(out=squares1[:, cols], in0=two1[:, cols], in1=ucd_sq1[c // 2][:, parts(4)[c % 2]], op=ALU.add)
            nc.scalar.activation(out=dev_b[1][:, cols], in_=squares1[:, cols], func=ACT.Sqrt, scale=1.0 / 3.0)

        def finish(half, mean_q, dev_q):
            cols = slice(half * VH, (half + 1) * VH)
            acc = psum.tile([P, VH], F32, name="acc%d" % half, tag="c%d" % half)
            for i, (codes, scales) in enumerate(((mean_q[0][:, cols], mean_q[1][:, cols]), (dev_q[0][:], dev_q[1][:]))):
                nc.tensor.matmul_mx(
                    out=acc[:],
                    lhsT=tail_words[i][:].bitcast(FP8X4),
                    lhsT_scale=tail_scales[i][:],
                    rhs=codes.bitcast(FP8X4),
                    rhs_scale=scales,
                    start=(i == 0),
                    stop=(i == 1),
                )
            result = keep.tile([P, VH], F32, name="result%d" % half)
            nc.scalar.copy(out=result[:], in_=acc[:])
            nc.sync.dma_start(out=out[:, cols], in_=result[:])

        means_q = quantize(mean_b[:].rearrange("p h v t -> p (h v t)"), 2 * VH, "mean", tag="ucd_sq1_0")
        dev0_q = quantize(dev_b[0][:].rearrange("p v t -> p (v t)"), VH, "dev0", tag="two1")
        finish(0, means_q, dev0_q)
        dev1_q = mx_tiles(VH, "dev1")
        for cols in parts(2):
            nc.vector.quantize_mx(
                out=dev1_q[0][:, cols].bitcast(FP8X4),
                scales=dev1_q[1][:, cols],
                in_=dev_b[1][:, cols].rearrange("p v t -> p (v t)"),
            )
        finish(1, means_q, dev1_q)
